import numpy as np
import ml_dtypes


def mxq(x, axis, fmt="e4m3"):
    dtype, down = {"e4m3": (ml_dtypes.float8_e4m3fn, 7), "e5m2": (ml_dtypes.float8_e5m2, 14)}[fmt]
    v = np.moveaxis(np.asarray(x, np.float32).astype(ml_dtypes.bfloat16).astype(np.float64), axis, -1)
    blocks = v.reshape(v.shape[:-1] + (-1, 32))
    amax = np.abs(blocks).max(-1, keepdims=True)
    byte = np.maximum(np.where(amax > 0, np.frexp(amax)[1] - 1 + 127, 0) - down, 1)
    scale = np.exp2(byte - 127.0)
    codes = (blocks / scale).astype(np.float32).astype(dtype).astype(np.float64)
    return np.moveaxis((codes * scale).reshape(v.shape), -1, axis)


WIDE = False


def mx_kscale(k):
    if not WIDE:
        return np.ones(k)
    levels = np.array([10, -10, 5, -5, 0])
    if k % 512:
        return np.exp2(np.random.permutation(np.resize(levels, k // 32))).repeat(32)
    a = np.empty((k // 512, 16))
    for p in range(k // 512):
        a[p, :8] = np.random.permutation(np.resize(levels, 8))
        for g in range(8):
            far = levels[np.abs(levels - a[p, g]) >= 10]
            a[p, g + 8] = far[np.random.randint(len(far))]
    return np.exp2(a.ravel()).repeat(32)


def f64(x):
    return np.asarray(x).astype(np.float64)


def striped(idx):
    return np.tile(idx.reshape(-1, 16).T, (8, 1)).astype(np.uint16)


def unstriped(offs):
    return offs[:16].T.reshape(-1).astype(np.int64)


K, T, S, N, U = 512, 2048, 1024, 256, 1024


def setup_inputs():
    n = np.random.standard_normal
    s = mx_kscale(K)[:, None]
    return {
        "xT": (n((K, T)) * s).astype(np.float32),
        "w1": (n((K, N)) / np.sqrt(K) / s).astype(np.float32),
        "w2": (n((K, N)) / np.sqrt(K) / s).astype(np.float32),
        "w3": (n((K, N)) / np.sqrt(K) / s).astype(np.float32),
        "offs": striped(np.random.permutation(T)[:S]),
        "src": striped(np.random.permutation(S)[(S * np.random.uniform(0, 1, U) ** 4).astype(np.int64)]),
        "dst": striped(np.random.permutation(S)),
    }


def reference(xT, w1, w2, w3, offs, src, dst):
    xq = mxq(f64(xT)[:, unstriped(offs)], 0, "e4m3")
    y = mxq(f64(w1), 0, "e4m3").T @ xq
    e = mxq(f64(w2), 0, "e4m3").T @ xq
    h = mxq(f64(w3), 0, "e4m3").T @ xq
    return (np.tanh(y[:, unstriped(dst)] + e[:, unstriped(src)])) * h[:, unstriped(src)]

@@ -1,0 +1,158 @@
+from contextlib import ExitStack
+
+import concourse.mybir as mybir
+
+K, T, S, N, U = 512, 2048, 1024, 256, 1024
+FLOPS = 3 * 2 * K * N * S
+
+F32 = mybir.dt.float32
+BF16 = mybir.dt.bfloat16
+U32 = mybir.dt.uint32
+U16 = mybir.dt.uint16
+U8 = mybir.dt.uint8
+FP8X4 = mybir.dt.float8_e4m3fn_x4
+ADD = mybir.AluOpType.add
+MULT = mybir.AluOpType.mult
+TANH = mybir.ActivationFunctionType.Tanh
+
+P = 128
+PACK = 4
+LIST_ROWS = 16
+BANK = 512
+
+CHUNKS = [
+    [(0, 1024), (1024, 2048)],
+    [(0, 1024), (1024, 1536), (1536, 1792), (1792, 2048)],
+]
+SHARED = 1696
+PIECE = 256
+EDGES = [[(0, 512), (512, 1024)], [(0, 512), (512, 768), (768, 1024)]]
+
+
+def entries(lst, lo, hi):
+    return lst[:, lo // LIST_ROWS : hi // LIST_ROWS]
+
+
+def tile_picked_edgeatt_tanh_e_kernel(tc, xT, w1, w2, w3, offs, src, dst, out):
+    nc = tc.nc
+    with ExitStack() as ctx:
+        keep = ctx.enter_context(tc.tile_pool(name="keep", bufs=1))
+        psum = ctx.enter_context(tc.psum_pool(name="psum", bufs=1))
+
+        offs_t = keep.tile([P, S // LIST_ROWS], U16, name="offs_t")
+        src_t = keep.tile([P, U // LIST_ROWS], U16, name="src_t")
+        dst_t = keep.tile([P, U // LIST_ROWS], U16, name="dst_t")
+
+        warm_in = keep.tile([P, 8], F32, name="warm_in")
+        warm_out = keep.tile([P, 8], F32, name="warm_out")
+        nc.gpsimd.memset(warm_in[:], 0.0)
+        nc.scalar.activation(warm_out[:], warm_in[:], TANH)
+
+        x_rows = xT.rearrange("(p j) t -> p j t", j=PACK)
+        raw = {}
+        for u in range(2):
+            for c, (lo, hi) in enumerate(CHUNKS[u]):
+                raw[u, c] = keep.tile([P, 2, hi - lo], F32, name="raw%d_%d" % (u, c))
+                nc.sync.dma_start(out=raw[u, c][:], in_=x_rows[:, 2 * u : 2 * u + 2, lo:hi])
+                if u == 0 and c == 0:
+                    nc.sync.dma_start(offs_t[:], offs)
+        w_raw = []
+        for i, w in enumerate((w1, w2, w3)):
+            w_raw.append(keep.tile([P, PACK, N], F32, name="w_raw%d" % i, tag="w_raw%d" % i, align_bytes=64))
+            nc.sync.dma_start(out=w_raw[i][:], in_=w.rearrange("(p j) n -> p j n", j=PACK))
+        nc.sync.dma_start(dst_t[:], dst)
+        nc.sync.dma_start(src_t[:], src)
+
+        pairs = [keep.tile([P, T], U32, name="pairs%d" % u) for u in range(2)]
+        picked = keep.tile([P, 2 * S], U32, name="picked", align_bytes=64)
+        x_scales = keep.tile([P, S], U8, name="x_scales", align_bytes=64)
+        w_bf = [keep.tile([P, N * PACK], BF16, name="w_bf%d" % i, align_bytes=64) for i in range(3)]
+        w_codes = [keep.tile([P, N], U32, name="w_codes%d" % i, align_bytes=64) for i in range(3)]
+        w_scales = [keep.tile([P, N], U8, name="w_scales%d" % i, align_bytes=64) for i in range(3)]
+        res = {(i, b): keep.tile([P, S], F32, name="res%d_%d" % (i, b)) for i in range(3) for b in range(2) if (i, b) != (0, 0)}
+
+        def cast(u, c, lo, hi, on_vector):
+            first = CHUNKS[u][c][0]
+            dst_view = pairs[u][:, lo:hi].bitcast(BF16).rearrange("p (t e) -> p t e", e=2)
+            src_view = raw[u, c][:, :, lo - first : hi - first].rearrange("p e t -> p t e")
+            if on_vector:
+                nc.vector.tensor_copy(out=dst_view, in_=src_view)
+            else:
+                nc.scalar.copy(out=dst_view, in_=src_view)
+
+        def pick(u):
+            slot = picked[:].rearrange("p (n u) -> p n u", u=2)[:, :, u]
+            nc.vector.tensor_copy(out=slot, in_=pairs[u][:].indirect(offs_t[:]))
+
+        def quantise_x(lo, hi):
+            nc.vector.quantize_mx(
+                out=x_codes[:, lo:hi].bitcast(FP8X4), scales=x_scales[:, lo:hi], in_=picked[:, 2 * lo : 2 * hi].bitcast(BF16)
+            )
+
+        def interleave_w(i):
+            nc.scalar.copy(
+                out=w_bf[i][:].rearrange("p (c n j) -> p c j n", n=4, j=PACK),
+                in_=w_raw[i][:].rearrange("p j (c n) -> p c j n", n=4),
+            )
+
+        def quantise_w(i):
+            nc.vector.quantize_mx(out=w_codes[i][:].bitcast(FP8X4), scales=w_scales[i][:], in_=w_bf[i][:])
+
+        def product(i, b, lo, hi, tag, bufs):
+            acc = psum.tile([P, hi - lo], F32, name="acc", tag=tag, bufs=bufs)
+            rows = slice(b * P, (b + 1) * P)
+            nc.tensor.matmul_mx(
+                out=acc[:],
+                lhsT=w_codes[i][:, rows].bitcast(FP8X4),
+                lhsT_scale=w_scales[i][:, rows],
+                rhs=x_codes[:, lo:hi].bitcast(FP8X4),
+                rhs_scale=x_scales[:, lo:hi],
+                start=True,
+                stop=True,
+            )
+            nc.scalar.copy(out=res[i, b][:, lo:hi], in_=acc[:])
+
+        def products(i, b):
+            for lo in range(0, S, BANK):
+                product(i, b, lo, lo + BANK, "ring", 4)
+
+        cast(0, 0, 0, 1024, True)
+        cast(0, 1, 1024, SHARED, True)
+        cast(0, 1, SHARED, T, False)
+        pick(0)
+        cast(1, 0, 0, 1024, False)
+        for c in range(1, 4):
+            cast(1, c, CHUNKS[1][c][0], CHUNKS[1][c][1], True)
+        pick(1)
+
+        for i in range(3):
+            interleave_w(i)
+        x_codes = keep.tile([P, S], U32, name="x_codes", tag="w_raw0", align_bytes=64)
+        res[0, 0] = keep.tile([P, S], F32, name="res0_0", tag="w_raw2", align_bytes=64)
+        quantise_w(0)
+        for lo in range(0, S, PIECE):
+            quantise_x(lo, lo + PIECE)
+            product(0, 0, lo, lo + PIECE, "first", 4)
+        quantise_w(1)
+        quantise_w(2)
+        products(1, 0)
+        products(2, 0)
+
+        for b in range(2):
+            y, e, h = res[0, b], res[1, b], res[2, b]
+            at_dst, summed, gate = {}, {}, {}
+            for lo, hi in EDGES[b]:
+                at_dst[lo] = keep.tile([P, hi - lo], F32, name="at_dst%d_%d" % (b, lo))
+                nc.vector.tensor_copy(out=at_dst[lo][:], in_=y[:].indirect(entries(dst_t, lo, hi)))
+            for lo, hi in EDGES[b]:
+                summed[lo] = keep.tile([P, hi - lo], F32, name="summed%d_%d" % (b, lo))
+                gate[lo] = keep.tile([P, hi - lo], F32, name="gate%d_%d" % (b, lo))
+                nc.vector.tensor_tensor(summed[lo][:], e[:].indirect(entries(src_t, lo, hi)), at_dst[lo][:], ADD)
+                nc.scalar.activation(gate[lo][:], summed[lo][:], TANH)
+            if b == 0:
+                for i in range(3):
+                    products(i, 1)
+            for lo, hi in EDGES[b]:
+                message = keep.tile([P, hi - lo], F32, name="message%d_%d" % (b, lo))
+                nc.vector.tensor_tensor(message[:], h[:].indirect(entries(src_t, lo, hi)), gate[lo][:], MULT)
+                nc.sync.dma_start(out=out[b * P : (b + 1) * P, lo:hi], in_=message[:])

@@ -8,6 +8,7 @@ FLOPS = 3 * 2 * K * N * S
 F32 = mybir.dt.float32
 BF16 = mybir.dt.bfloat16
 U32 = mybir.dt.uint32
+I32 = mybir.dt.int32
 U16 = mybir.dt.uint16
 U8 = mybir.dt.uint8
 FP8X4 = mybir.dt.float8_e4m3fn_x4
@@ -26,6 +27,7 @@ CHUNKS = [
 ]
 SHARED = 1696
 PIECE = 256
+PICKS = [(0, 256), (256, 640), (640, 1024)]
 EDGES = [[(0, 512), (512, 1024)], [(0, 512), (512, 768), (768, 1024)]]
 
 
@@ -64,7 +66,8 @@ def tile_picked_edgeatt_tanh_e_kernel(tc, xT, w1, w2, w3, offs, src, dst, out):
         nc.sync.dma_start(src_t[:], src)
 
         pairs = [keep.tile([P, T], U32, name="pairs%d" % u) for u in range(2)]
-        picked = keep.tile([P, 2 * S], U32, name="picked", align_bytes=64)
+        picked = [keep.tile([P, 2, hi - lo], U32, name="picked%d" % i) for i, (lo, hi) in enumerate(PICKS)]
+        woven = keep.tile([P, 2 * S], U32, name="woven", align_bytes=64)
         x_scales = keep.tile([P, S], U8, name="x_scales", align_bytes=64)
         w_bf = [keep.tile([P, N * PACK], BF16, name="w_bf%d" % i, align_bytes=64) for i in range(3)]
         w_codes = [keep.tile([P, N], U32, name="w_codes%d" % i, align_bytes=64) for i in range(3)]
@@ -80,13 +83,26 @@ def tile_picked_edgeatt_tanh_e_kernel(tc, xT, w1, w2, w3, offs, src, dst, out):
             else:
                 nc.scalar.copy(out=dst_view, in_=src_view)
 
-        def pick(u):
-            slot = picked[:].rearrange("p (n u) -> p n u", u=2)[:, :, u]
-            nc.vector.tensor_copy(out=slot, in_=pairs[u][:].indirect(offs_t[:]))
+        def pick(u, i):
+            lo, hi = PICKS[i]
+            nc.vector.tensor_copy(out=picked[i][:, u, :], in_=pairs[u][:].indirect(entries(offs_t, lo, hi)))
+
+        def weave(i, on_vector):
+            lo, hi = PICKS[i]
+            if on_vector:
+                nc.vector.tensor_copy(
+                    out=woven[:, 2 * lo : 2 * hi].bitcast(I32).rearrange("p (n u) -> p n u", u=2),
+                    in_=picked[i][:].bitcast(I32).rearrange("p u n -> p n u"),
+                )
+            else:
+                nc.scalar.copy(
+                    out=woven[:, 2 * lo : 2 * hi].rearrange("p (n u) -> p n u", u=2),
+                    in_=picked[i][:].rearrange("p u n -> p n u"),
+                )
 
         def quantise_x(lo, hi):
             nc.vector.quantize_mx(
-                out=x_codes[:, lo:hi].bitcast(FP8X4), scales=x_scales[:, lo:hi], in_=picked[:, 2 * lo : 2 * hi].bitcast(BF16)
+                out=x_codes[:, lo:hi].bitcast(FP8X4), scales=x_scales[:, lo:hi], in_=woven[:, 2 * lo : 2 * hi].bitcast(BF16)
             )
 
         def interleave_w(i):
@@ -119,40 +135,64 @@ def tile_picked_edgeatt_tanh_e_kernel(tc, xT, w1, w2, w3, offs, src, dst, out):
         cast(0, 0, 0, 1024, True)
         cast(0, 1, 1024, SHARED, True)
         cast(0, 1, SHARED, T, False)
-        pick(0)
-        cast(1, 0, 0, 1024, False)
+        for i in range(3):
+            pick(0, i)
+        cast(1, 0, 0, 768, False)
+        cast(1, 0, 768, 1024, True)
         for c in range(1, 4):
             cast(1, c, CHUNKS[1][c][0], CHUNKS[1][c][1], True)
-        pick(1)
+        pick(1, 0)
+        weave(0, False)
+        pick(1, 1)
+        pick(1, 2)
+        weave(1, True)
+        weave(2, True)
 
-        for i in range(3):
-            interleave_w(i)
+        interleave_w(0)
+        interleave_w(1)
         x_codes = keep.tile([P, S], U32, name="x_codes", tag="w_raw0", align_bytes=64)
-        res[0, 0] = keep.tile([P, S], F32, name="res0_0", tag="w_raw2", align_bytes=64)
+        res[0, 0] = keep.tile([P, S], F32, name="res0_0", tag="w_raw1", align_bytes=64)
         quantise_w(0)
         for lo in range(0, S, PIECE):
             quantise_x(lo, lo + PIECE)
             product(0, 0, lo, lo + PIECE, "first", 4)
         quantise_w(1)
-        quantise_w(2)
-        products(1, 0)
-        products(2, 0)
 
-        for b in range(2):
-            y, e, h = res[0, b], res[1, b], res[2, b]
-            at_dst, summed, gate = {}, {}, {}
+        at_dst, summed, gate = {}, {}, {}
+
+        def fetch_dst(b):
             for lo, hi in EDGES[b]:
-                at_dst[lo] = keep.tile([P, hi - lo], F32, name="at_dst%d_%d" % (b, lo))
-                nc.vector.tensor_copy(out=at_dst[lo][:], in_=y[:].indirect(entries(dst_t, lo, hi)))
+                at_dst[b, lo] = keep.tile([P, hi - lo], F32, name="at_dst%d_%d" % (b, lo))
+                nc.vector.tensor_copy(out=at_dst[b, lo][:], in_=res[0, b][:].indirect(entries(dst_t, lo, hi)))
+
+        def add_src(b):
             for lo, hi in EDGES[b]:
-                summed[lo] = keep.tile([P, hi - lo], F32, name="summed%d_%d" % (b, lo))
-                gate[lo] = keep.tile([P, hi - lo], F32, name="gate%d_%d" % (b, lo))
-                nc.vector.tensor_tensor(summed[lo][:], e[:].indirect(entries(src_t, lo, hi)), at_dst[lo][:], ADD)
-                nc.scalar.activation(gate[lo][:], summed[lo][:], TANH)
-            if b == 0:
-                for i in range(3):
-                    products(i, 1)
+                summed[b, lo] = keep.tile([P, hi - lo], F32, name="summed%d_%d" % (b, lo))
+                nc.vector.tensor_tensor(summed[b, lo][:], res[1, b][:].indirect(entries(src_t, lo, hi)), at_dst[b, lo][:], ADD)
+
+        def squash(b):
+            for lo, hi in EDGES[b]:
+                gate[b, lo] = keep.tile([P, hi - lo], F32, name="gate%d_%d" % (b, lo))
+                nc.scalar.activation(gate[b, lo][:], summed[b, lo][:], TANH)
+
+        def send(b):
             for lo, hi in EDGES[b]:
                 message = keep.tile([P, hi - lo], F32, name="message%d_%d" % (b, lo))
-                nc.vector.tensor_tensor(message[:], h[:].indirect(entries(src_t, lo, hi)), gate[lo][:], MULT)
+                nc.vector.tensor_tensor(message[:], res[2, b][:].indirect(entries(src_t, lo, hi)), gate[b, lo][:], MULT)
                 nc.sync.dma_start(out=out[b * P : (b + 1) * P, lo:hi], in_=message[:])
+
+        products(1, 0)
+        fetch_dst(0)
+        add_src(0)
+        interleave_w(2)
+        quantise_w(2)
+        products(0, 1)
+        squash(0)
+        fetch_dst(1)
+        products(2, 0)
+        products(1, 1)
+        send(0)
+        add_src(1)
+        products(2, 1)
+        squash(1)
+        send(1)

@@ -27,8 +27,12 @@ CHUNKS = [
 ]
 SHARED = 1696
 PIECE = 256
-PICKS = [(0, 256), (256, 640), (640, 1024)]
-EDGES = [[(0, 512), (512, 1024)], [(0, 512), (512, 768), (768, 1024)]]
+PICKS = [(0, 256), (256, 512), (512, 768), (768, 1024)]
+SPARE = [352, 16, 16]
+W_PARTS = [(0, 0, 128), (0, 128, 256), (1, 0, 256), (2, 0, 256)]
+HALVES = [(0, 512), (512, 1024)]
+WHOLE = [(0, 1024)]
+LAST = [(0, 512), (512, 768), (768, 1024)]
 
 
 def entries(lst, lo, hi):
@@ -39,16 +43,12 @@ def tile_picked_edgeatt_tanh_e_kernel(tc, xT, w1, w2, w3, offs, src, dst, out):
     nc = tc.nc
     with ExitStack() as ctx:
         keep = ctx.enter_context(tc.tile_pool(name="keep", bufs=1))
+        shared = ctx.enter_context(tc.tile_pool(name="shared", bufs=1))
         psum = ctx.enter_context(tc.psum_pool(name="psum", bufs=1))
 
         offs_t = keep.tile([P, S // LIST_ROWS], U16, name="offs_t")
         src_t = keep.tile([P, U // LIST_ROWS], U16, name="src_t")
         dst_t = keep.tile([P, U // LIST_ROWS], U16, name="dst_t")
-
-        warm_in = keep.tile([P, 8], F32, name="warm_in")
-        warm_out = keep.tile([P, 8], F32, name="warm_out")
-        nc.gpsimd.memset(warm_in[:], 0.0)
-        nc.scalar.activation(warm_out[:], warm_in[:], TANH)
 
         x_rows = xT.rearrange("(p j) t -> p j t", j=PACK)
         raw = {}
@@ -59,20 +59,34 @@ def tile_picked_edgeatt_tanh_e_kernel(tc, xT, w1, w2, w3, offs, src, dst, out):
                 if u == 0 and c == 0:
                     nc.sync.dma_start(offs_t[:], offs)
         w_raw = []
-        for i, w in enumerate((w1, w2, w3)):
-            w_raw.append(keep.tile([P, PACK, N], F32, name="w_raw%d" % i, tag="w_raw%d" % i, align_bytes=64))
-            nc.sync.dma_start(out=w_raw[i][:], in_=w.rearrange("(p j) n -> p j n", j=PACK))
+        for part, (i, lo, hi) in enumerate(W_PARTS):
+            w_rows = (w1, w2, w3)[i].rearrange("(p j) n -> p j n", j=PACK)
+            if part == 0:
+                w_raw.append(shared.tile([P, PACK, hi - lo], F32, name="w_raw0", offset=1024, align_bytes=64))
+            else:
+                w_raw.append(keep.tile([P, PACK, hi - lo], F32, name="w_raw%d" % part))
+            nc.sync.dma_start(out=w_raw[part][:], in_=w_rows[:, :, lo:hi])
         nc.sync.dma_start(dst_t[:], dst)
         nc.sync.dma_start(src_t[:], src)
 
         pairs = [keep.tile([P, T], U32, name="pairs%d" % u) for u in range(2)]
-        picked = [keep.tile([P, 2, hi - lo], U32, name="picked%d" % i) for i, (lo, hi) in enumerate(PICKS)]
-        woven = keep.tile([P, 2 * S], U32, name="woven", align_bytes=64)
+        picked = [keep.tile([P, 2, hi - lo], U32, name="picked%d" % i, tag="picked%d" % i, align_bytes=64) for i, (lo, hi) in enumerate(PICKS)]
+        woven = {}
+        x_codes = keep.tile([P, S], U32, name="x_codes", align_bytes=64)
         x_scales = keep.tile([P, S], U8, name="x_scales", align_bytes=64)
-        w_bf = [keep.tile([P, N * PACK], BF16, name="w_bf%d" % i, align_bytes=64) for i in range(3)]
+        w_bf = {
+            part: keep.tile([P, (hi - lo) * PACK], BF16, name="w_bf%d" % part, align_bytes=64)
+            for part, (i, lo, hi) in enumerate(W_PARTS)
+            if part == 0
+        }
         w_codes = [keep.tile([P, N], U32, name="w_codes%d" % i, align_bytes=64) for i in range(3)]
         w_scales = [keep.tile([P, N], U8, name="w_scales%d" % i, align_bytes=64) for i in range(3)]
-        res = {(i, b): keep.tile([P, S], F32, name="res%d_%d" % (i, b)) for i in range(3) for b in range(2) if (i, b) != (0, 0)}
+        res = {(i, b): keep.tile([P, S + SPARE[i]], F32, name="res%d_%d" % (i, b)) for i in range(3) for b in range(2)}
+        zeros = keep.tile([P, max(SPARE)], F32, name="zeros")
+        nc.gpsimd.memset(zeros[:], 0.0)
+        for i in range(3):
+            for b in range(2):
+                nc.scalar.activation(res[i, b][:, S:], zeros[:, : SPARE[i]], TANH)
 
         def cast(u, c, lo, hi, on_vector):
             first = CHUNKS[u][c][0]
@@ -88,31 +102,34 @@ def tile_picked_edgeatt_tanh_e_kernel(tc, xT, w1, w2, w3, offs, src, dst, out):
             nc.vector.tensor_copy(out=picked[i][:, u, :], in_=pairs[u][:].indirect(entries(offs_t, lo, hi)))
 
         def weave(i, on_vector):
-            lo, hi = PICKS[i]
             if on_vector:
                 nc.vector.tensor_copy(
-                    out=woven[:, 2 * lo : 2 * hi].bitcast(I32).rearrange("p (n u) -> p n u", u=2),
+                    out=woven[i].bitcast(I32).rearrange("p (n u) -> p n u", u=2),
                     in_=picked[i][:].bitcast(I32).rearrange("p u n -> p n u"),
                 )
             else:
                 nc.scalar.copy(
-                    out=woven[:, 2 * lo : 2 * hi].rearrange("p (n u) -> p n u", u=2),
+                    out=woven[i].rearrange("p (n u) -> p n u", u=2),
                     in_=picked[i][:].rearrange("p u n -> p n u"),
                 )
 
-        def quantise_x(lo, hi):
+        def quantise_x(i):
+            lo, hi = PICKS[i]
             nc.vector.quantize_mx(
-                out=x_codes[:, lo:hi].bitcast(FP8X4), scales=x_scales[:, lo:hi], in_=woven[:, 2 * lo : 2 * hi].bitcast(BF16)
+                out=x_codes[:, lo:hi].bitcast(FP8X4), scales=x_scales[:, lo:hi], in_=woven[i].bitcast(BF16)
             )
 
-        def interleave_w(i):
-            nc.scalar.copy(
-                out=w_bf[i][:].rearrange("p (c n j) -> p c j n", n=4, j=PACK),
-                in_=w_raw[i][:].rearrange("p j (c n) -> p c j n", n=4),
-            )
+        def interleave_w(i, on_vector):
+            grouped = w_bf[i][:].rearrange("p (c n j) -> p c j n", n=4, j=PACK)
+            planes = w_raw[i][:].rearrange("p j (c n) -> p c j n", n=4)
+            if on_vector:
+                nc.vector.tensor_copy(out=grouped, in_=planes)
+            else:
+                nc.scalar.copy(out=grouped, in_=planes)
 
-        def quantise_w(i):
-            nc.vector.quantize_mx(out=w_codes[i][:].bitcast(FP8X4), scales=w_scales[i][:], in_=w_bf[i][:])
+        def quantise_w(part):
+            i, lo, hi = W_PARTS[part]
+            nc.vector.quantize_mx(out=w_codes[i][:, lo:hi].bitcast(FP8X4), scales=w_scales[i][:, lo:hi], in_=w_bf[part][:])
 
         def product(i, b, lo, hi, tag, bufs):
             acc = psum.tile([P, hi - lo], F32, name="acc", tag=tag, bufs=bufs)
@@ -135,64 +152,65 @@ def tile_picked_edgeatt_tanh_e_kernel(tc, xT, w1, w2, w3, offs, src, dst, out):
         cast(0, 0, 0, 1024, True)
         cast(0, 1, 1024, SHARED, True)
         cast(0, 1, SHARED, T, False)
-        for i in range(3):
+        for i in range(4):
             pick(0, i)
         cast(1, 0, 0, 768, False)
         cast(1, 0, 768, 1024, True)
         for c in range(1, 4):
             cast(1, c, CHUNKS[1][c][0], CHUNKS[1][c][1], True)
-        pick(1, 0)
-        weave(0, False)
-        pick(1, 1)
-        pick(1, 2)
-        weave(1, True)
-        weave(2, True)
-
-        interleave_w(0)
-        interleave_w(1)
-        x_codes = keep.tile([P, S], U32, name="x_codes", tag="w_raw0", align_bytes=64)
-        res[0, 0] = keep.tile([P, S], F32, name="res0_0", tag="w_raw1", align_bytes=64)
+        interleave_w(0, False)
+        for i in range(4):
+            pick(1, i)
+        for i in range(2):
+            woven[i] = shared.tile([P, 2 * PIECE], U32, name="woven%d" % i, offset=2048 * i, align_bytes=64)[:]
+            weave(i, False)
+        for i in range(2, 4):
+            woven[i] = keep.tile([P, 2 * PIECE], U32, name="woven%d" % i, tag="picked%d" % (i - 2), align_bytes=64)[:]
+            weave(i, False)
+        w_bf[1] = keep.tile([P, P * PACK], BF16, name="w_bf1", tag="picked2", align_bytes=64)
+        interleave_w(1, False)
         quantise_w(0)
-        for lo in range(0, S, PIECE):
-            quantise_x(lo, lo + PIECE)
-            product(0, 0, lo, lo + PIECE, "first", 4)
+        for i in range(4):
+            lo, hi = PICKS[i]
+            quantise_x(i)
+            product(0, 0, lo, hi, "first", 4)
+        w_bf[2] = keep.tile([P, N * PACK], BF16, name="w_bf2", tag="picked1", align_bytes=64)
+        interleave_w(2, True)
         quantise_w(1)
+        quantise_w(2)
 
-        at_dst, summed, gate = {}, {}, {}
+        at_dst = [keep.tile([P, U], F32, name="at_dst%d" % b) for b in range(2)]
+        summed = [keep.tile([P, U], F32, name="summed%d" % b) for b in range(2)]
+        gate = [keep.tile([P, U], F32, name="gate%d" % b) for b in range(2)]
 
         def fetch_dst(b):
-            for lo, hi in EDGES[b]:
-                at_dst[b, lo] = keep.tile([P, hi - lo], F32, name="at_dst%d_%d" % (b, lo))
-                nc.vector.tensor_copy(out=at_dst[b, lo][:], in_=res[0, b][:].indirect(entries(dst_t, lo, hi)))
+            nc.vector.tensor_copy(out=at_dst[b][:], in_=res[0, b][:].indirect(dst_t[:]))
 
         def add_src(b):
-            for lo, hi in EDGES[b]:
-                summed[b, lo] = keep.tile([P, hi - lo], F32, name="summed%d_%d" % (b, lo))
-                nc.vector.tensor_tensor(summed[b, lo][:], res[1, b][:].indirect(entries(src_t, lo, hi)), at_dst[b, lo][:], ADD)
+            nc.vector.tensor_tensor(summed[b][:], res[1, b][:].indirect(src_t[:]), at_dst[b][:], ADD)
 
         def squash(b):
-            for lo, hi in EDGES[b]:
-                gate[b, lo] = keep.tile([P, hi - lo], F32, name="gate%d_%d" % (b, lo))
-                nc.scalar.activation(gate[b, lo][:], summed[b, lo][:], TANH)
+            nc.scalar.activation(gate[b][:], summed[b][:], TANH)
 
-        def send(b):
-            for lo, hi in EDGES[b]:
+        def send(b, pieces):
+            for lo, hi in pieces:
                 message = keep.tile([P, hi - lo], F32, name="message%d_%d" % (b, lo))
-                nc.vector.tensor_tensor(message[:], res[2, b][:].indirect(entries(src_t, lo, hi)), gate[b, lo][:], MULT)
+                nc.vector.tensor_tensor(message[:], res[2, b][:].indirect(entries(src_t, lo, hi)), gate[b][:, lo:hi], MULT)
                 nc.sync.dma_start(out=out[b * P : (b + 1) * P, lo:hi], in_=message[:])
 
-        products(1, 0)
         fetch_dst(0)
-        add_src(0)
-        interleave_w(2)
-        quantise_w(2)
         products(0, 1)
-        squash(0)
         fetch_dst(1)
-        products(2, 0)
+        products(1, 0)
+        add_src(0)
+        w_bf[3] = keep.tile([P, N * PACK], BF16, name="w_bf3", tag="picked1", align_bytes=64)
+        interleave_w(3, False)
+        quantise_w(3)
         products(1, 1)
-        send(0)
         add_src(1)
+        squash(0)
+        products(2, 0)
+        send(0, WHOLE)
         products(2, 1)
         squash(1)
-        send(1)
+        send(1, LAST)

@@ -22,17 +22,19 @@ LIST_ROWS = 16
 BANK = 512
 
 CHUNKS = [
-    [(0, 1024), (1024, 2048)],
+    [(0, 1024), (1024, 1536), (1536, 2048)],
     [(0, 1024), (1024, 1536), (1536, 1792), (1792, 2048)],
 ]
-SHARED = 1696
+SHARED = 1872
 PIECE = 256
 PICKS = [(0, 256), (256, 512), (512, 768), (768, 1024)]
+WEAVES = [(0, 256), (256, 512), (512, 768), (768, 896), (896, 1024)]
 SPARE = [352, 16, 16]
-W_PARTS = [(0, 0, 128), (0, 128, 256), (1, 0, 256), (2, 0, 256)]
+W_LOADS = [(0, 0, 128), (0, 128, 256), (1, 0, 256), (2, 0, 256)]
+W_PARTS = [(0, 0, 128), (0, 128, 256), (1, 0, 128), (1, 128, 256), (2, 0, 256)]
 HALVES = [(0, 512), (512, 1024)]
 WHOLE = [(0, 1024)]
-LAST = [(0, 512), (512, 768), (768, 1024)]
+LAST = [(0, 512), (512, 768), (768, 896), (896, 1024)]
 
 
 def entries(lst, lo, hi):
@@ -59,18 +61,21 @@ def tile_picked_edgeatt_tanh_e_kernel(tc, xT, w1, w2, w3, offs, src, dst, out):
                 if u == 0 and c == 0:
                     nc.sync.dma_start(offs_t[:], offs)
         w_raw = []
-        for part, (i, lo, hi) in enumerate(W_PARTS):
+        for part, (i, lo, hi) in enumerate(W_LOADS):
             w_rows = (w1, w2, w3)[i].rearrange("(p j) n -> p j n", j=PACK)
             if part == 0:
-                w_raw.append(shared.tile([P, PACK, hi - lo], F32, name="w_raw0", offset=1024, align_bytes=64))
+                wide = shared.tile([P, PACK, 4 * (hi - lo)], F32, name="w_raw0", offset=0, align_bytes=64)
+                w_raw.append(wide[:, :, : hi - lo])
             else:
-                w_raw.append(keep.tile([P, PACK, hi - lo], F32, name="w_raw%d" % part))
-            nc.sync.dma_start(out=w_raw[part][:], in_=w_rows[:, :, lo:hi])
+                w_raw.append(keep.tile([P, PACK, hi - lo], F32, name="w_raw%d" % part)[:])
+            nc.sync.dma_start(out=w_raw[part], in_=w_rows[:, :, lo:hi])
+        w_raw = [w_raw[0], w_raw[1], w_raw[2][:, :, :P], w_raw[2][:, :, P:], w_raw[3]]
         nc.sync.dma_start(dst_t[:], dst)
         nc.sync.dma_start(src_t[:], src)
 
         pairs = [keep.tile([P, T], U32, name="pairs%d" % u) for u in range(2)]
-        picked = [keep.tile([P, 2, hi - lo], U32, name="picked%d" % i, tag="picked%d" % i, align_bytes=64) for i, (lo, hi) in enumerate(PICKS)]
+        picked_all = shared.tile([P, len(PICKS), 2, PIECE], U32, name="picked_all", offset=8192, align_bytes=64)
+        picked = [picked_all[:, i, :, :] for i in range(len(PICKS))]
         woven = {}
         x_codes = keep.tile([P, S], U32, name="x_codes", align_bytes=64)
         x_scales = keep.tile([P, S], U8, name="x_scales", align_bytes=64)
@@ -101,27 +106,20 @@ def tile_picked_edgeatt_tanh_e_kernel(tc, xT, w1, w2, w3, offs, src, dst, out):
             lo, hi = PICKS[i]
             nc.vector.tensor_copy(out=picked[i][:, u, :], in_=pairs[u][:].indirect(entries(offs_t, lo, hi)))
 
-        def weave(i, on_vector):
-            if on_vector:
-                nc.vector.tensor_copy(
-                    out=woven[i].bitcast(I32).rearrange("p (n u) -> p n u", u=2),
-                    in_=picked[i][:].bitcast(I32).rearrange("p u n -> p n u"),
-                )
-            else:
-                nc.scalar.copy(
-                    out=woven[i].rearrange("p (n u) -> p n u", u=2),
-                    in_=picked[i][:].rearrange("p u n -> p n u"),
-                )
+        def weave(i):
+            lo, hi = WEAVES[i]
+            piece = picked[lo // PIECE][:, :, lo % PIECE : lo % PIECE + hi - lo]
+            nc.scalar.copy(out=woven[i].rearrange("p (n u) -> p n u", u=2), in_=piece.rearrange("p u n -> p n u"))
 
         def quantise_x(i):
-            lo, hi = PICKS[i]
+            lo, hi = WEAVES[i]
             nc.vector.quantize_mx(
                 out=x_codes[:, lo:hi].bitcast(FP8X4), scales=x_scales[:, lo:hi], in_=woven[i].bitcast(BF16)
             )
 
         def interleave_w(i, on_vector):
             grouped = w_bf[i][:].rearrange("p (c n j) -> p c j n", n=4, j=PACK)
-            planes = w_raw[i][:].rearrange("p j (c n) -> p c j n", n=4)
+            planes = w_raw[i].rearrange("p j (c n) -> p c j n", n=4)
             if on_vector:
                 nc.vector.tensor_copy(out=grouped, in_=planes)
             else:
@@ -147,34 +145,32 @@ def tile_picked_edgeatt_tanh_e_kernel(tc, xT, w1, w2, w3, offs, src, dst, out):
 
         def products(i, b):
             for lo in range(0, S, BANK):
-                product(i, b, lo, lo + BANK, "ring", 4)
+                product(i, b, lo, lo + BANK, "ring", 8)
 
         cast(0, 0, 0, 1024, True)
-        cast(0, 1, 1024, SHARED, True)
-        cast(0, 1, SHARED, T, False)
-        for i in range(4):
-            pick(0, i)
-        cast(1, 0, 0, 768, False)
-        cast(1, 0, 768, 1024, True)
-        for c in range(1, 4):
+        cast(0, 1, 1024, 1536, True)
+        cast(0, 2, 1536, SHARED, True)
+        cast(0, 2, SHARED, T, False)
+        nc.vector.tensor_copy(out=picked_all[:, :, 0, :], in_=pairs[0][:].indirect(offs_t[:]))
+        cast(1, 0, 0, 896, False)
+        cast(1, 0, 896, 1024, True)
+        for c in range(1, 3):
             cast(1, c, CHUNKS[1][c][0], CHUNKS[1][c][1], True)
+        cast(1, 3, 1792, 1960, True)
+        cast(1, 3, 1960, T, False)
         interleave_w(0, False)
         for i in range(4):
             pick(1, i)
-        for i in range(2):
-            woven[i] = shared.tile([P, 2 * PIECE], U32, name="woven%d" % i, offset=2048 * i, align_bytes=64)[:]
-            weave(i, False)
-        for i in range(2, 4):
-            woven[i] = keep.tile([P, 2 * PIECE], U32, name="woven%d" % i, tag="picked%d" % (i - 2), align_bytes=64)[:]
-            weave(i, False)
-        w_bf[1] = keep.tile([P, P * PACK], BF16, name="w_bf1", tag="picked2", align_bytes=64)
-        interleave_w(1, False)
+        for i, (lo, hi) in enumerate(WEAVES):
+            woven[i] = shared.tile([P, 2 * (hi - lo)], U32, name="woven%d" % i, offset=8 * lo, align_bytes=64)[:]
+            weave(i)
         quantise_w(0)
-        for i in range(4):
-            lo, hi = PICKS[i]
+        for i, (lo, hi) in enumerate(WEAVES):
             quantise_x(i)
-            product(0, 0, lo, hi, "first", 4)
-        w_bf[2] = keep.tile([P, N * PACK], BF16, name="w_bf2", tag="picked1", align_bytes=64)
+            product(0, 0, lo, hi, "ring", 8)
+        w_bf[1] = shared.tile([P, P * PACK], BF16, name="w_bf1", offset=8192, align_bytes=64)
+        interleave_w(1, True)
+        w_bf[2] = shared.tile([P, P * PACK], BF16, name="w_bf2", offset=8192 + 2048, align_bytes=64)
         interleave_w(2, True)
         quantise_w(1)
         quantise_w(2)
@@ -200,12 +196,15 @@ def tile_picked_edgeatt_tanh_e_kernel(tc, xT, w1, w2, w3, offs, src, dst, out):
 
         fetch_dst(0)
         products(0, 1)
+        w_bf[3] = shared.tile([P, P * PACK], BF16, name="w_bf3", offset=8192, align_bytes=64)
+        interleave_w(3, False)
+        w_bf[4] = shared.tile([P, N * PACK], BF16, name="w_bf4", offset=8192 + 2048, align_bytes=64)
+        interleave_w(4, False)
         fetch_dst(1)
+        quantise_w(3)
+        quantise_w(4)
         products(1, 0)
         add_src(0)
-        w_bf[3] = keep.tile([P, N * PACK], BF16, name="w_bf3", tag="picked1", align_bytes=64)
-        interleave_w(3, False)
-        quantise_w(3)
         products(1, 1)
         add_src(1)
         squash(0)

@@ -22,10 +22,9 @@ LIST_ROWS = 16
 BANK = 512
 
 CHUNKS = [
-    [(0, 1024), (1024, 1536), (1536, 2048)],
-    [(0, 1024), (1024, 1536), (1536, 1792), (1792, 2048)],
+    [(0, 928, 1408), (1408, 1832, 2048)],
+    [(0, 544, 1152), (1152, 1576, 1792), (1792, 1960, 2048)],
 ]
-SHARED = 1872
 PIECE = 256
 PICKS = [(0, 256), (256, 512), (512, 768), (768, 1024)]
 WEAVES = [(0, 256), (256, 512), (512, 768), (768, 896), (896, 1024)]
@@ -55,7 +54,7 @@ def tile_picked_edgeatt_tanh_e_kernel(tc, xT, w1, w2, w3, offs, src, dst, out):
         x_rows = xT.rearrange("(p j) t -> p j t", j=PACK)
         raw = {}
         for u in range(2):
-            for c, (lo, hi) in enumerate(CHUNKS[u]):
+            for c, (lo, cut, hi) in enumerate(CHUNKS[u]):
                 raw[u, c] = keep.tile([P, 2, hi - lo], F32, name="raw%d_%d" % (u, c))
                 nc.sync.dma_start(out=raw[u, c][:], in_=x_rows[:, 2 * u : 2 * u + 2, lo:hi])
                 if u == 0 and c == 0:
@@ -147,17 +146,14 @@ def tile_picked_edgeatt_tanh_e_kernel(tc, xT, w1, w2, w3, offs, src, dst, out):
             for lo in range(0, S, BANK):
                 product(i, b, lo, lo + BANK, "ring", 8)
 
-        cast(0, 0, 0, 1024, True)
-        cast(0, 1, 1024, 1536, True)
-        cast(0, 2, 1536, SHARED, True)
-        cast(0, 2, SHARED, T, False)
+        def cast_pair(u):
+            for c, (lo, cut, hi) in enumerate(CHUNKS[u]):
+                cast(u, c, lo, cut, True)
+                cast(u, c, cut, hi, False)
+
+        cast_pair(0)
         nc.vector.tensor_copy(out=picked_all[:, :, 0, :], in_=pairs[0][:].indirect(offs_t[:]))
-        cast(1, 0, 0, 896, False)
-        cast(1, 0, 896, 1024, True)
-        for c in range(1, 3):
-            cast(1, c, CHUNKS[1][c][0], CHUNKS[1][c][1], True)
-        cast(1, 3, 1792, 1960, True)
-        cast(1, 3, 1960, T, False)
+        cast_pair(1)
         interleave_w(0, False)
         for i in range(4):
             pick(1, i)

@@ -22,15 +22,15 @@ LIST_ROWS = 16
 BANK = 512
 
 CHUNKS = [
-    [(0, 928, 1408), (1408, 1832, 2048)],
-    [(0, 544, 1152), (1152, 1576, 1792), (1792, 1960, 2048)],
+    [(0, 1024, 1024), (1024, 1664, 1664), (1664, 1920, 2048)],
+    [(0, 0, 640), (640, 1040, 1280), (1280, 1624, 1792), (1792, 1960, 2048)],
 ]
 PIECE = 256
 PICKS = [(0, 256), (256, 512), (512, 768), (768, 1024)]
 WEAVES = [(0, 256), (256, 512), (512, 768), (768, 896), (896, 1024)]
 SPARE = [352, 16, 16]
 W_LOADS = [(0, 0, 128), (0, 128, 256), (1, 0, 256), (2, 0, 256)]
-W_PARTS = [(0, 0, 128), (0, 128, 256), (1, 0, 128), (1, 128, 256), (2, 0, 256)]
+W_PARTS = [(0, 0, 128), (0, 128, 256), (1, 0, 256), (2, 0, 256)]
 HALVES = [(0, 512), (512, 1024)]
 WHOLE = [(0, 1024)]
 LAST = [(0, 512), (512, 768), (768, 896), (896, 1024)]
@@ -68,7 +68,6 @@ def tile_picked_edgeatt_tanh_e_kernel(tc, xT, w1, w2, w3, offs, src, dst, out):
             else:
                 w_raw.append(keep.tile([P, PACK, hi - lo], F32, name="w_raw%d" % part)[:])
             nc.sync.dma_start(out=w_raw[part], in_=w_rows[:, :, lo:hi])
-        w_raw = [w_raw[0], w_raw[1], w_raw[2][:, :, :P], w_raw[2][:, :, P:], w_raw[3]]
         nc.sync.dma_start(dst_t[:], dst)
         nc.sync.dma_start(src_t[:], src)
 
@@ -83,8 +82,8 @@ def tile_picked_edgeatt_tanh_e_kernel(tc, xT, w1, w2, w3, offs, src, dst, out):
             for part, (i, lo, hi) in enumerate(W_PARTS)
             if part == 0
         }
-        w_codes = [keep.tile([P, N], U32, name="w_codes%d" % i, align_bytes=64) for i in range(3)]
-        w_scales = [keep.tile([P, N], U8, name="w_scales%d" % i, align_bytes=64) for i in range(3)]
+        w_codes = {}
+        w_scales = {}
         res = {(i, b): keep.tile([P, S + SPARE[i]], F32, name="res%d_%d" % (i, b)) for i in range(3) for b in range(2)}
         zeros = keep.tile([P, max(SPARE)], F32, name="zeros")
         nc.gpsimd.memset(zeros[:], 0.0)
@@ -116,25 +115,34 @@ def tile_picked_edgeatt_tanh_e_kernel(tc, xT, w1, w2, w3, offs, src, dst, out):
                 out=x_codes[:, lo:hi].bitcast(FP8X4), scales=x_scales[:, lo:hi], in_=woven[i].bitcast(BF16)
             )
 
-        def interleave_w(i, on_vector):
+        def interleave_w(i, on_vector, on_pool=False):
             grouped = w_bf[i][:].rearrange("p (c n j) -> p c j n", n=4, j=PACK)
             planes = w_raw[i].rearrange("p j (c n) -> p c j n", n=4)
-            if on_vector:
+            if on_pool:
+                nc.gpsimd.tensor_scalar(grouped, planes, 1.0, 0.0, MULT, ADD)
+            elif on_vector:
                 nc.vector.tensor_copy(out=grouped, in_=planes)
             else:
                 nc.scalar.copy(out=grouped, in_=planes)
 
         def quantise_w(part):
             i, lo, hi = W_PARTS[part]
-            nc.vector.quantize_mx(out=w_codes[i][:, lo:hi].bitcast(FP8X4), scales=w_scales[i][:, lo:hi], in_=w_bf[part][:])
+            if part == 1:
+                codes = shared.tile([P, hi - lo], U32, name="w_codes1", offset=8192, align_bytes=64)
+            else:
+                codes = keep.tile([P, hi - lo], U32, name="w_codes%d" % part, align_bytes=64)
+            scales = keep.tile([P, hi - lo], U8, name="w_scales%d" % part, align_bytes=64)
+            nc.vector.quantize_mx(out=codes[:].bitcast(FP8X4), scales=scales[:], in_=w_bf[part][:])
+            for first in range(lo, hi, P):
+                w_codes[i, first // P] = codes[:, first - lo : first - lo + P]
+                w_scales[i, first // P] = scales[:, first - lo : first - lo + P]
 
         def product(i, b, lo, hi, tag, bufs):
             acc = psum.tile([P, hi - lo], F32, name="acc", tag=tag, bufs=bufs)
-            rows = slice(b * P, (b + 1) * P)
             nc.tensor.matmul_mx(
                 out=acc[:],
-                lhsT=w_codes[i][:, rows].bitcast(FP8X4),
-                lhsT_scale=w_scales[i][:, rows],
+                lhsT=w_codes[i, b].bitcast(FP8X4),
+                lhsT_scale=w_scales[i, b],
                 rhs=x_codes[:, lo:hi].bitcast(FP8X4),
                 rhs_scale=x_scales[:, lo:hi],
                 start=True,
@@ -148,13 +156,17 @@ def tile_picked_edgeatt_tanh_e_kernel(tc, xT, w1, w2, w3, offs, src, dst, out):
 
         def cast_pair(u):
             for c, (lo, cut, hi) in enumerate(CHUNKS[u]):
-                cast(u, c, lo, cut, True)
-                cast(u, c, cut, hi, False)
+                if cut > lo:
+                    cast(u, c, lo, cut, True)
+                if hi > cut:
+                    cast(u, c, cut, hi, False)
 
         cast_pair(0)
         nc.vector.tensor_copy(out=picked_all[:, :, 0, :], in_=pairs[0][:].indirect(offs_t[:]))
         cast_pair(1)
         interleave_w(0, False)
+        w_bf[1] = keep.tile([P, P * PACK], BF16, name="w_bf1", align_bytes=64)
+        interleave_w(1, False, True)
         for i in range(4):
             pick(1, i)
         for i, (lo, hi) in enumerate(WEAVES):
@@ -164,9 +176,7 @@ def tile_picked_edgeatt_tanh_e_kernel(tc, xT, w1, w2, w3, offs, src, dst, out):
         for i, (lo, hi) in enumerate(WEAVES):
             quantise_x(i)
             product(0, 0, lo, hi, "ring", 8)
-        w_bf[1] = shared.tile([P, P * PACK], BF16, name="w_bf1", offset=8192, align_bytes=64)
-        interleave_w(1, True)
-        w_bf[2] = shared.tile([P, P * PACK], BF16, name="w_bf2", offset=8192 + 2048, align_bytes=64)
+        w_bf[2] = shared.tile([P, N * PACK], BF16, name="w_bf2", offset=8192 + 2048, align_bytes=64)
         interleave_w(2, True)
         quantise_w(1)
         quantise_w(2)
@@ -192,13 +202,10 @@ def tile_picked_edgeatt_tanh_e_kernel(tc, xT, w1, w2, w3, offs, src, dst, out):
 
         fetch_dst(0)
         products(0, 1)
-        w_bf[3] = shared.tile([P, P * PACK], BF16, name="w_bf3", offset=8192, align_bytes=64)
+        w_bf[3] = shared.tile([P, N * PACK], BF16, name="w_bf3", offset=8192 + 2048, align_bytes=64)
         interleave_w(3, False)
-        w_bf[4] = shared.tile([P, N * PACK], BF16, name="w_bf4", offset=8192 + 2048, align_bytes=64)
-        interleave_w(4, False)
         fetch_dst(1)
         quantise_w(3)
-        quantise_w(4)
         products(1, 0)
         add_src(0)
         products(1, 1)

@@ -8,7 +8,6 @@ FLOPS = 3 * 2 * K * N * S
 F32 = mybir.dt.float32
 BF16 = mybir.dt.bfloat16
 U32 = mybir.dt.uint32
-I32 = mybir.dt.int32
 U16 = mybir.dt.uint16
 U8 = mybir.dt.uint8
 FP8X4 = mybir.dt.float8_e4m3fn_x4
@@ -22,18 +21,18 @@ LIST_ROWS = 16
 BANK = 512
 
 CHUNKS = [
-    [(0, 1024, 1024), (1024, 1664, 1664), (1664, 1920, 2048)],
-    [(0, 0, 640), (640, 1040, 1280), (1280, 1624, 1792), (1792, 1960, 2048)],
+    [(0, 1536), (1536, 2048)],
+    [(0, 640), (640, 1280), (1280, 1792), (1792, 2048)],
 ]
 PIECE = 256
-PICKS = [(0, 256), (256, 512), (512, 768), (768, 1024)]
-WEAVES = [(0, 256), (256, 512), (512, 768), (768, 896), (896, 1024)]
+STEPS = [(0, 256), (256, 512), (512, 768), (768, 896), (896, 1024)]
 SPARE = [352, 16, 16]
-W_LOADS = [(0, 0, 128), (0, 128, 256), (1, 0, 256), (2, 0, 256)]
 W_PARTS = [(0, 0, 128), (0, 128, 256), (1, 0, 256), (2, 0, 256)]
-HALVES = [(0, 512), (512, 1024)]
-WHOLE = [(0, 1024)]
 LAST = [(0, 512), (512, 768), (768, 896), (896, 1024)]
+
+WOVEN_BYTES = 8
+PICKED_AT = WOVEN_BYTES * S
+W_BF_AT = PICKED_AT + 4 * PACK * P
 
 
 def entries(lst, lo, hi):
@@ -54,17 +53,17 @@ def tile_picked_edgeatt_tanh_e_kernel(tc, xT, w1, w2, w3, offs, src, dst, out):
         x_rows = xT.rearrange("(p j) t -> p j t", j=PACK)
         raw = {}
         for u in range(2):
-            for c, (lo, cut, hi) in enumerate(CHUNKS[u]):
+            for c, (lo, hi) in enumerate(CHUNKS[u]):
                 raw[u, c] = keep.tile([P, 2, hi - lo], F32, name="raw%d_%d" % (u, c))
                 nc.sync.dma_start(out=raw[u, c][:], in_=x_rows[:, 2 * u : 2 * u + 2, lo:hi])
                 if u == 0 and c == 0:
                     nc.sync.dma_start(offs_t[:], offs)
         w_raw = []
-        for part, (i, lo, hi) in enumerate(W_LOADS):
+        for part, (i, lo, hi) in enumerate(W_PARTS):
             w_rows = (w1, w2, w3)[i].rearrange("(p j) n -> p j n", j=PACK)
             if part == 0:
-                wide = shared.tile([P, PACK, 4 * (hi - lo)], F32, name="w_raw0", offset=0, align_bytes=64)
-                w_raw.append(wide[:, :, : hi - lo])
+                span = shared.tile([P, PACK, PICKED_AT // (4 * PACK)], F32, name="w_raw0", offset=0, align_bytes=64)
+                w_raw.append(span[:, :, : hi - lo])
             else:
                 w_raw.append(keep.tile([P, PACK, hi - lo], F32, name="w_raw%d" % part)[:])
             nc.sync.dma_start(out=w_raw[part], in_=w_rows[:, :, lo:hi])
@@ -72,16 +71,12 @@ def tile_picked_edgeatt_tanh_e_kernel(tc, xT, w1, w2, w3, offs, src, dst, out):
         nc.sync.dma_start(src_t[:], src)
 
         pairs = [keep.tile([P, T], U32, name="pairs%d" % u) for u in range(2)]
-        picked_all = shared.tile([P, len(PICKS), 2, PIECE], U32, name="picked_all", offset=8192, align_bytes=64)
-        picked = [picked_all[:, i, :, :] for i in range(len(PICKS))]
+        picked = shared.tile([P, S // PIECE, 2, PIECE], U32, name="picked_all", offset=PICKED_AT, align_bytes=64)
         woven = {}
         x_codes = keep.tile([P, S], U32, name="x_codes", align_bytes=64)
         x_scales = keep.tile([P, S], U8, name="x_scales", align_bytes=64)
-        w_bf = {
-            part: keep.tile([P, (hi - lo) * PACK], BF16, name="w_bf%d" % part, align_bytes=64)
-            for part, (i, lo, hi) in enumerate(W_PARTS)
-            if part == 0
-        }
+        w_bf = {}
+        w_bf_first = keep.tile([P, PACK * P], BF16, name="w_bf0", align_bytes=64)
         w_codes = {}
         w_scales = {}
         res = {(i, b): keep.tile([P, S + SPARE[i]], F32, name="res%d_%d" % (i, b)) for i in range(3) for b in range(2)}
@@ -91,54 +86,45 @@ def tile_picked_edgeatt_tanh_e_kernel(tc, xT, w1, w2, w3, offs, src, dst, out):
             for b in range(2):
                 nc.scalar.activation(res[i, b][:, S:], zeros[:, : SPARE[i]], TANH)
 
-        def cast(u, c, lo, hi, on_vector):
-            first = CHUNKS[u][c][0]
-            dst_view = pairs[u][:, lo:hi].bitcast(BF16).rearrange("p (t e) -> p t e", e=2)
-            src_view = raw[u, c][:, :, lo - first : hi - first].rearrange("p e t -> p t e")
-            if on_vector:
-                nc.vector.tensor_copy(out=dst_view, in_=src_view)
-            else:
-                nc.scalar.copy(out=dst_view, in_=src_view)
+        def cast(u, c, vector_share):
+            lo, hi = CHUNKS[u][c]
+            cut = round(vector_share * (hi - lo) / 8) * 8
+            words = pairs[u][:, lo:hi].bitcast(BF16).rearrange("p (t e) -> p t e", e=2)
+            rows = raw[u, c][:].rearrange("p e t -> p t e")
+            if cut > 0:
+                nc.vector.tensor_copy(out=words[:, :cut, :], in_=rows[:, :cut, :])
+            if cut < hi - lo:
+                nc.scalar.copy(out=words[:, cut:, :], in_=rows[:, cut:, :])
 
-        def pick(u, i):
-            lo, hi = PICKS[i]
-            nc.vector.tensor_copy(out=picked[i][:, u, :], in_=pairs[u][:].indirect(entries(offs_t, lo, hi)))
+        def weave(step):
+            lo, hi = STEPS[step]
+            woven[step] = shared.tile(
+                [P, 2 * (hi - lo)], U32, name="woven%d" % step, offset=WOVEN_BYTES * lo, align_bytes=64
+            )
+            words = picked[:, lo // PIECE, :, lo % PIECE : lo % PIECE + hi - lo]
+            nc.scalar.copy(out=woven[step][:].rearrange("p (n u) -> p n u", u=2), in_=words.rearrange("p u n -> p n u"))
 
-        def weave(i):
-            lo, hi = WEAVES[i]
-            piece = picked[lo // PIECE][:, :, lo % PIECE : lo % PIECE + hi - lo]
-            nc.scalar.copy(out=woven[i].rearrange("p (n u) -> p n u", u=2), in_=piece.rearrange("p u n -> p n u"))
-
-        def quantise_x(i):
-            lo, hi = WEAVES[i]
+        def quantise_x(step):
+            lo, hi = STEPS[step]
             nc.vector.quantize_mx(
-                out=x_codes[:, lo:hi].bitcast(FP8X4), scales=x_scales[:, lo:hi], in_=woven[i].bitcast(BF16)
+                out=x_codes[:, lo:hi].bitcast(FP8X4), scales=x_scales[:, lo:hi], in_=woven[step][:].bitcast(BF16)
             )
 
-        def interleave_w(i, on_vector, on_pool=False):
-            grouped = w_bf[i][:].rearrange("p (c n j) -> p c j n", n=4, j=PACK)
-            planes = w_raw[i].rearrange("p j (c n) -> p c j n", n=4)
-            if on_pool:
-                nc.gpsimd.tensor_scalar(grouped, planes, 1.0, 0.0, MULT, ADD)
-            elif on_vector:
-                nc.vector.tensor_copy(out=grouped, in_=planes)
-            else:
-                nc.scalar.copy(out=grouped, in_=planes)
+        def interleave_views(part, tile):
+            w_bf[part] = tile
+            grouped = tile[:].rearrange("p (c n j) -> p c j n", n=4, j=PACK)
+            return grouped, w_raw[part].rearrange("p j (c n) -> p c j n", n=4)
 
-        def quantise_w(part):
+        def quantise_w(part, codes):
             i, lo, hi = W_PARTS[part]
-            if part == 1:
-                codes = shared.tile([P, hi - lo], U32, name="w_codes1", offset=8192, align_bytes=64)
-            else:
-                codes = keep.tile([P, hi - lo], U32, name="w_codes%d" % part, align_bytes=64)
             scales = keep.tile([P, hi - lo], U8, name="w_scales%d" % part, align_bytes=64)
             nc.vector.quantize_mx(out=codes[:].bitcast(FP8X4), scales=scales[:], in_=w_bf[part][:])
             for first in range(lo, hi, P):
                 w_codes[i, first // P] = codes[:, first - lo : first - lo + P]
                 w_scales[i, first // P] = scales[:, first - lo : first - lo + P]
 
-        def product(i, b, lo, hi, tag, bufs):
-            acc = psum.tile([P, hi - lo], F32, name="acc", tag=tag, bufs=bufs)
+        def product(i, b, lo, hi):
+            acc = psum.tile([P, hi - lo], F32, name="acc", tag="ring", bufs=8)
             nc.tensor.matmul_mx(
                 out=acc[:],
                 lhsT=w_codes[i, b].bitcast(FP8X4),
@@ -152,34 +138,36 @@ def tile_picked_edgeatt_tanh_e_kernel(tc, xT, w1, w2, w3, offs, src, dst, out):
 
         def products(i, b):
             for lo in range(0, S, BANK):
-                product(i, b, lo, lo + BANK, "ring", 8)
+                product(i, b, lo, lo + BANK)
 
-        def cast_pair(u):
-            for c, (lo, cut, hi) in enumerate(CHUNKS[u]):
-                if cut > lo:
-                    cast(u, c, lo, cut, True)
-                if hi > cut:
-                    cast(u, c, cut, hi, False)
+        both = 2 / 3
+        cast(0, 0, both)
+        cast(0, 1, both)
+        nc.vector.tensor_copy(out=picked[:, :, 0, :], in_=pairs[0][:].indirect(offs_t[:]))
+        cast(1, 0, 0)
+        cast(1, 1, 1 / 2)
+        cast(1, 2, both)
+        cast(1, 3, both)
 
-        cast_pair(0)
-        nc.vector.tensor_copy(out=picked_all[:, :, 0, :], in_=pairs[0][:].indirect(offs_t[:]))
-        cast_pair(1)
-        interleave_w(0, False)
-        w_bf[1] = keep.tile([P, P * PACK], BF16, name="w_bf1", align_bytes=64)
-        interleave_w(1, False, True)
-        for i in range(4):
-            pick(1, i)
-        for i, (lo, hi) in enumerate(WEAVES):
-            woven[i] = shared.tile([P, 2 * (hi - lo)], U32, name="woven%d" % i, offset=8 * lo, align_bytes=64)[:]
-            weave(i)
-        quantise_w(0)
-        for i, (lo, hi) in enumerate(WEAVES):
-            quantise_x(i)
-            product(0, 0, lo, hi, "ring", 8)
-        w_bf[2] = shared.tile([P, N * PACK], BF16, name="w_bf2", offset=8192 + 2048, align_bytes=64)
-        interleave_w(2, True)
-        quantise_w(1)
-        quantise_w(2)
+        nc.scalar.copy(*interleave_views(0, w_bf_first))
+        grouped, planes = interleave_views(1, keep.tile([P, PACK * P], BF16, name="w_bf1", align_bytes=64))
+        nc.gpsimd.tensor_scalar(grouped, planes, 1.0, 0.0, MULT, ADD)
+
+        for piece in range(S // PIECE):
+            picks = entries(offs_t, piece * PIECE, (piece + 1) * PIECE)
+            nc.vector.tensor_copy(out=picked[:, piece, 1, :], in_=pairs[1][:].indirect(picks))
+        for step in range(len(STEPS)):
+            weave(step)
+        quantise_w(0, keep.tile([P, P], U32, name="w_codes0", align_bytes=64))
+        for step, (lo, hi) in enumerate(STEPS):
+            quantise_x(step)
+            product(0, 0, lo, hi)
+
+        nc.vector.tensor_copy(
+            *interleave_views(2, shared.tile([P, PACK * N], BF16, name="w_bf2", offset=W_BF_AT, align_bytes=64))
+        )
+        quantise_w(1, shared.tile([P, P], U32, name="w_codes1", offset=PICKED_AT, align_bytes=64))
+        quantise_w(2, keep.tile([P, N], U32, name="w_codes2", align_bytes=64))
 
         at_dst = [keep.tile([P, U], F32, name="at_dst%d" % b) for b in range(2)]
         summed = [keep.tile([P, U], F32, name="summed%d" % b) for b in range(2)]
@@ -194,25 +182,26 @@ def tile_picked_edgeatt_tanh_e_kernel(tc, xT, w1, w2, w3, offs, src, dst, out):
         def squash(b):
             nc.scalar.activation(gate[b][:], summed[b][:], TANH)
 
-        def send(b, pieces):
-            for lo, hi in pieces:
+        def send(b, ranges):
+            for lo, hi in ranges:
                 message = keep.tile([P, hi - lo], F32, name="message%d_%d" % (b, lo))
                 nc.vector.tensor_tensor(message[:], res[2, b][:].indirect(entries(src_t, lo, hi)), gate[b][:, lo:hi], MULT)
                 nc.sync.dma_start(out=out[b * P : (b + 1) * P, lo:hi], in_=message[:])
 
         fetch_dst(0)
         products(0, 1)
-        w_bf[3] = shared.tile([P, N * PACK], BF16, name="w_bf3", offset=8192 + 2048, align_bytes=64)
-        interleave_w(3, False)
+        nc.scalar.copy(
+            *interleave_views(3, shared.tile([P, PACK * N], BF16, name="w_bf3", offset=W_BF_AT, align_bytes=64))
+        )
         fetch_dst(1)
-        quantise_w(3)
+        quantise_w(3, keep.tile([P, N], U32, name="w_codes3", align_bytes=64))
         products(1, 0)
         add_src(0)
         products(1, 1)
         add_src(1)
         squash(0)
         products(2, 0)
-        send(0, WHOLE)
+        send(0, [(0, U // 2), (U // 2, U)])
         products(2, 1)
         squash(1)
         send(1, LAST)

@@ -14,16 +14,13 @@ FP8X4 = mybir.dt.float8_e4m3fn_x4
 ADD = mybir.AluOpType.add
 MULT = mybir.AluOpType.mult
 TANH = mybir.ActivationFunctionType.Tanh
+COPY = mybir.ActivationFunctionType.Copy
 
 P = 128
 PACK = 4
 LIST_ROWS = 16
 BANK = 512
 
-CHUNKS = [
-    [(0, 1536), (1536, 2048)],
-    [(0, 640), (640, 1280), (1280, 1792), (1792, 2048)],
-]
 PIECE = 256
 STEPS = [(0, 256), (256, 512), (512, 768), (768, 896), (896, 1024)]
 SPARE = [352, 16, 16]
@@ -32,7 +29,7 @@ LAST = [(0, 512), (512, 768), (768, 896), (896, 1024)]
 
 WOVEN_BYTES = 8
 PICKED_AT = WOVEN_BYTES * S
-W_BF_AT = PICKED_AT + 4 * PACK * P
+W_BF_AT = PICKED_AT + 4 * P
 
 
 def entries(lst, lo, hi):
@@ -51,13 +48,11 @@ def tile_picked_edgeatt_tanh_e_kernel(tc, xT, w1, w2, w3, offs, src, dst, out):
         dst_t = keep.tile([P, U // LIST_ROWS], U16, name="dst_t")
 
         x_rows = xT.rearrange("(p j) t -> p j t", j=PACK)
-        raw = {}
-        for u in range(2):
-            for c, (lo, hi) in enumerate(CHUNKS[u]):
-                raw[u, c] = keep.tile([P, 2, hi - lo], F32, name="raw%d_%d" % (u, c))
-                nc.sync.dma_start(out=raw[u, c][:], in_=x_rows[:, 2 * u : 2 * u + 2, lo:hi])
-                if u == 0 and c == 0:
-                    nc.sync.dma_start(offs_t[:], offs)
+        rows = [keep.tile([P, T], F32, name="row%d" % j) for j in range(PACK)]
+        for j in (2, 0, 1, 3):
+            nc.sync.dma_start(out=rows[j][:], in_=x_rows[:, j, :])
+            if j == 2:
+                nc.sync.dma_start(offs_t[:], offs)
         w_raw = []
         for part, (i, lo, hi) in enumerate(W_PARTS):
             w_rows = (w1, w2, w3)[i].rearrange("(p j) n -> p j n", j=PACK)
@@ -70,8 +65,11 @@ def tile_picked_edgeatt_tanh_e_kernel(tc, xT, w1, w2, w3, offs, src, dst, out):
         nc.sync.dma_start(dst_t[:], dst)
         nc.sync.dma_start(src_t[:], src)
 
-        pairs = [keep.tile([P, T], U32, name="pairs%d" % u) for u in range(2)]
-        picked = shared.tile([P, S // PIECE, 2, PIECE], U32, name="picked_all", offset=PICKED_AT, align_bytes=64)
+        rows_bf = [keep.tile([P, T], BF16, name="row_bf%d" % j) for j in range(2)]
+        picked = [
+            shared.tile([P, 2, PIECE], U32, name="picked%d" % t, offset=PICKED_AT + 8 * PIECE * (3 - t), align_bytes=64)
+            for t in range(S // PIECE)
+        ]
         woven = {}
         x_codes = keep.tile([P, S], U32, name="x_codes", align_bytes=64)
         x_scales = keep.tile([P, S], U8, name="x_scales", align_bytes=64)
@@ -86,22 +84,12 @@ def tile_picked_edgeatt_tanh_e_kernel(tc, xT, w1, w2, w3, offs, src, dst, out):
             for b in range(2):
                 nc.scalar.activation(res[i, b][:, S:], zeros[:, : SPARE[i]], TANH)
 
-        def cast(u, c, vector_share):
-            lo, hi = CHUNKS[u][c]
-            cut = round(vector_share * (hi - lo) / 8) * 8
-            words = pairs[u][:, lo:hi].bitcast(BF16).rearrange("p (t e) -> p t e", e=2)
-            rows = raw[u, c][:].rearrange("p e t -> p t e")
-            if cut > 0:
-                nc.vector.tensor_copy(out=words[:, :cut, :], in_=rows[:, :cut, :])
-            if cut < hi - lo:
-                nc.scalar.copy(out=words[:, cut:, :], in_=rows[:, cut:, :])
-
         def weave(step):
             lo, hi = STEPS[step]
             woven[step] = shared.tile(
                 [P, 2 * (hi - lo)], U32, name="woven%d" % step, offset=WOVEN_BYTES * lo, align_bytes=64
             )
-            words = picked[:, lo // PIECE, :, lo % PIECE : lo % PIECE + hi - lo]
+            words = picked[lo // PIECE][:, :, lo % PIECE : lo % PIECE + hi - lo]
             nc.scalar.copy(out=woven[step][:].rearrange("p (n u) -> p n u", u=2), in_=words.rearrange("p u n -> p n u"))
 
         def quantise_x(step):
@@ -140,22 +128,29 @@ def tile_picked_edgeatt_tanh_e_kernel(tc, xT, w1, w2, w3, offs, src, dst, out):
             for lo in range(0, S, BANK):
                 product(i, b, lo, lo + BANK)
 
-        both = 2 / 3
-        cast(0, 0, both)
-        cast(0, 1, both)
-        nc.vector.tensor_copy(out=picked[:, :, 0, :], in_=pairs[0][:].indirect(offs_t[:]))
-        cast(1, 0, 0)
-        cast(1, 1, 1 / 2)
-        cast(1, 2, both)
-        cast(1, 3, both)
+        def picks(t):
+            return entries(offs_t, t * PIECE, (t + 1) * PIECE)
+
+        def slot(t, j):
+            return picked[t][:, j // 2, :].bitcast(BF16).rearrange("p (n e) -> p n e", e=2)[:, :, j % 2]
+
+        for t in range(S // PIECE):
+            nc.vector.tensor_copy(out=slot(t, 2), in_=rows[2][:].indirect(picks(t)))
+        cut = T // 2
+        for j in range(2):
+            nc.vector.tensor_copy(out=rows_bf[j][:, :cut], in_=rows[j][:, :cut])
+            nc.scalar.copy(out=rows_bf[j][:, cut:], in_=rows[j][:, cut:])
+            for t in (0, 1):
+                nc.vector.tensor_copy(out=slot(t, j), in_=rows[j][:].indirect(picks(t)))
+            for t in (2, 3):
+                nc.scalar.activation(slot(t, j), rows_bf[j][:].indirect(picks(t)), COPY)
 
         nc.scalar.copy(*interleave_views(0, w_bf_first))
         grouped, planes = interleave_views(1, keep.tile([P, PACK * P], BF16, name="w_bf1", align_bytes=64))
         nc.gpsimd.tensor_scalar(grouped, planes, 1.0, 0.0, MULT, ADD)
 
         for piece in range(S // PIECE):
-            picks = entries(offs_t, piece * PIECE, (piece + 1) * PIECE)
-            nc.vector.tensor_copy(out=picked[:, piece, 1, :], in_=pairs[1][:].indirect(picks))
+            nc.vector.tensor_copy(out=slot(piece, 3), in_=rows[3][:].indirect(picks(piece)))
         for step in range(len(STEPS)):
             weave(step)
         quantise_w(0, keep.tile([P, P], U32, name="w_codes0", align_bytes=64))

@@ -21,11 +21,11 @@ PACK = 4
 LIST_ROWS = 16
 BANK = 512
 
-PIECE = 256
+PIECES = [(0, 512), (512, 768), (768, 1024)]
 STEPS = [(0, 256), (256, 512), (512, 768), (768, 896), (896, 1024)]
 SPARE = [352, 16, 16]
 W_PARTS = [(0, 0, 128), (0, 128, 256), (1, 0, 256), (2, 0, 256)]
-LAST = [(0, 512), (512, 768), (768, 896), (896, 1024)]
+LAST = [(0, 640), (640, 896), (896, 1024)]
 
 WOVEN_BYTES = 8
 PICKED_AT = WOVEN_BYTES * S
@@ -49,9 +49,10 @@ def tile_picked_edgeatt_tanh_e_kernel(tc, xT, w1, w2, w3, offs, src, dst, out):
 
         x_rows = xT.rearrange("(p j) t -> p j t", j=PACK)
         rows = [keep.tile([P, T], F32, name="row%d" % j) for j in range(PACK)]
-        for j in (2, 0, 1, 3):
-            nc.sync.dma_start(out=rows[j][:], in_=x_rows[:, j, :])
-            if j == 2:
+        for j in (0, 2, 1, 3):
+            for lo, hi in [(0, 1024), (1024, T)] if j == 1 else [(0, T)]:
+                nc.sync.dma_start(out=rows[j][:, lo:hi], in_=x_rows[:, j, lo:hi])
+            if j == 0:
                 nc.sync.dma_start(offs_t[:], offs)
         w_raw = []
         for part, (i, lo, hi) in enumerate(W_PARTS):
@@ -67,8 +68,8 @@ def tile_picked_edgeatt_tanh_e_kernel(tc, xT, w1, w2, w3, offs, src, dst, out):
 
         rows_bf = [keep.tile([P, T], BF16, name="row_bf%d" % j) for j in range(2)]
         picked = [
-            shared.tile([P, 2, PIECE], U32, name="picked%d" % t, offset=PICKED_AT + 8 * PIECE * (3 - t), align_bytes=64)
-            for t in range(S // PIECE)
+            shared.tile([P, 2, hi - lo], U32, name="picked%d" % lo, offset=PICKED_AT + 8 * (S - hi), align_bytes=64)
+            for lo, hi in PIECES
         ]
         woven = {}
         x_codes = keep.tile([P, S], U32, name="x_codes", align_bytes=64)
@@ -89,7 +90,8 @@ def tile_picked_edgeatt_tanh_e_kernel(tc, xT, w1, w2, w3, offs, src, dst, out):
             woven[step] = shared.tile(
                 [P, 2 * (hi - lo)], U32, name="woven%d" % step, offset=WOVEN_BYTES * lo, align_bytes=64
             )
-            words = picked[lo // PIECE][:, :, lo % PIECE : lo % PIECE + hi - lo]
+            t = max(t for t, piece in enumerate(PIECES) if piece[0] <= lo)
+            words = picked[t][:, :, lo - PIECES[t][0] : hi - PIECES[t][0]]
             nc.scalar.copy(out=woven[step][:].rearrange("p (n u) -> p n u", u=2), in_=words.rearrange("p u n -> p n u"))
 
         def quantise_x(step):
@@ -129,27 +131,29 @@ def tile_picked_edgeatt_tanh_e_kernel(tc, xT, w1, w2, w3, offs, src, dst, out):
                 product(i, b, lo, lo + BANK)
 
         def picks(t):
-            return entries(offs_t, t * PIECE, (t + 1) * PIECE)
+            return entries(offs_t, *PIECES[t])
 
         def slot(t, j):
             return picked[t][:, j // 2, :].bitcast(BF16).rearrange("p (n e) -> p n e", e=2)[:, :, j % 2]
 
-        for t in range(S // PIECE):
-            nc.vector.tensor_copy(out=slot(t, 2), in_=rows[2][:].indirect(picks(t)))
-        cut = T // 2
         for j in range(2):
-            nc.vector.tensor_copy(out=rows_bf[j][:, :cut], in_=rows[j][:, :cut])
-            nc.scalar.copy(out=rows_bf[j][:, cut:], in_=rows[j][:, cut:])
-            for t in (0, 1):
+            cut = (768, 1536)[j]
+            for lo, hi in [(0, 1024), (1024, cut)] if j == 1 else [(0, cut)]:
+                nc.scalar.copy(out=rows_bf[j][:, lo:hi], in_=rows[j][:, lo:hi])
+            nc.vector.tensor_copy(out=rows_bf[j][:, cut:], in_=rows[j][:, cut:])
+            for t in (0,):
                 nc.vector.tensor_copy(out=slot(t, j), in_=rows[j][:].indirect(picks(t)))
-            for t in (2, 3):
+            for t in (1, 2):
                 nc.scalar.activation(slot(t, j), rows_bf[j][:].indirect(picks(t)), COPY)
+            if j == 0:
+                for t in range(len(PIECES)):
+                    nc.vector.tensor_copy(out=slot(t, 2), in_=rows[2][:].indirect(picks(t)))
 
         nc.scalar.copy(*interleave_views(0, w_bf_first))
         grouped, planes = interleave_views(1, keep.tile([P, PACK * P], BF16, name="w_bf1", align_bytes=64))
         nc.gpsimd.tensor_scalar(grouped, planes, 1.0, 0.0, MULT, ADD)
 
-        for piece in range(S // PIECE):
+        for piece in range(len(PIECES)):
             nc.vector.tensor_copy(out=slot(piece, 3), in_=rows[3][:].indirect(picks(piece)))
         for step in range(len(STEPS)):
             weave(step)
@@ -196,7 +200,7 @@ def tile_picked_edgeatt_tanh_e_kernel(tc, xT, w1, w2, w3, offs, src, dst, out):
         add_src(1)
         squash(0)
         products(2, 0)
-        send(0, [(0, U // 2), (U // 2, U)])
+        send(0, [(0, U)])
         products(2, 1)
         squash(1)
         send(1, LAST)

@@ -21,15 +21,13 @@ PACK = 4
 LIST_ROWS = 16
 BANK = 512
 
-PIECES = [(0, 512), (512, 768), (768, 1024)]
-STEPS = [(0, 256), (256, 512), (512, 768), (768, 896), (896, 1024)]
-SPARE = [352, 16, 16]
-W_PARTS = [(0, 0, 128), (0, 128, 256), (1, 0, 256), (2, 0, 256)]
-LAST = [(0, 640), (640, 896), (896, 1024)]
-
-WOVEN_BYTES = 8
-PICKED_AT = WOVEN_BYTES * S
-W_BF_AT = PICKED_AT + 4 * P
+DIRECT = 256
+STEPS = [(0, 256), (256, 512), (512, 768), (768, 1024)]
+HALVES = [(0, 512), (512, 1024)]
+THIRDS = [(0, 384), (384, 768), (768, 1024)]
+LAST = [(0, 384), (384, 768), (768, 896), (896, 1024)]
+SPARE = 16
+W_GROUPS = [[(0, 0)], [(1, 0)], [(2, 0), (0, 1)], [(1, 1), (2, 1)]]
 
 
 def entries(lst, lo, hi):
@@ -40,7 +38,6 @@ def tile_picked_edgeatt_tanh_e_kernel(tc, xT, w1, w2, w3, offs, src, dst, out):
     nc = tc.nc
     with ExitStack() as ctx:
         keep = ctx.enter_context(tc.tile_pool(name="keep", bufs=1))
-        shared = ctx.enter_context(tc.tile_pool(name="shared", bufs=1))
         psum = ctx.enter_context(tc.psum_pool(name="psum", bufs=1))
 
         offs_t = keep.tile([P, S // LIST_ROWS], U16, name="offs_t")
@@ -49,158 +46,163 @@ def tile_picked_edgeatt_tanh_e_kernel(tc, xT, w1, w2, w3, offs, src, dst, out):
 
         x_rows = xT.rearrange("(p j) t -> p j t", j=PACK)
         rows = [keep.tile([P, T], F32, name="row%d" % j) for j in range(PACK)]
-        for j in (0, 2, 1, 3):
-            for lo, hi in [(0, 1024), (1024, T)] if j == 1 else [(0, T)]:
-                nc.sync.dma_start(out=rows[j][:, lo:hi], in_=x_rows[:, j, lo:hi])
+        for j in range(PACK):
+            nc.sync.dma_start(out=rows[j][:], in_=x_rows[:, j, :])
             if j == 0:
                 nc.sync.dma_start(offs_t[:], offs)
         w_raw = []
-        for part, (i, lo, hi) in enumerate(W_PARTS):
-            w_rows = (w1, w2, w3)[i].rearrange("(p j) n -> p j n", j=PACK)
-            if part == 0:
-                span = shared.tile([P, PACK, PICKED_AT // (4 * PACK)], F32, name="w_raw0", offset=0, align_bytes=64)
-                w_raw.append(span[:, :, : hi - lo])
-            else:
-                w_raw.append(keep.tile([P, PACK, hi - lo], F32, name="w_raw%d" % part)[:])
-            nc.sync.dma_start(out=w_raw[part], in_=w_rows[:, :, lo:hi])
+        for i, w in enumerate((w1, w2, w3)):
+            w_raw.append(keep.tile([P, PACK, N], F32, name="w_raw%d" % i))
+            nc.sync.dma_start(out=w_raw[i][:], in_=w.rearrange("(p j) n -> p j n", j=PACK))
         nc.sync.dma_start(dst_t[:], dst)
         nc.sync.dma_start(src_t[:], src)
 
-        rows_bf = [keep.tile([P, T], BF16, name="row_bf%d" % j) for j in range(2)]
-        picked = [
-            shared.tile([P, 2, hi - lo], U32, name="picked%d" % lo, offset=PICKED_AT + 8 * (S - hi), align_bytes=64)
-            for lo, hi in PIECES
-        ]
-        woven = {}
+        x_bf = keep.tile([P, PACK * S], BF16, name="x_bf", align_bytes=64)
+        x_slots = x_bf[:].rearrange("p (n j) -> p n j", j=PACK)
         x_codes = keep.tile([P, S], U32, name="x_codes", align_bytes=64)
         x_scales = keep.tile([P, S], U8, name="x_scales", align_bytes=64)
-        w_bf = {}
-        w_bf_first = keep.tile([P, PACK * P], BF16, name="w_bf0", align_bytes=64)
-        w_codes = {}
-        w_scales = {}
-        res = {(i, b): keep.tile([P, S + SPARE[i]], F32, name="res%d_%d" % (i, b)) for i in range(3) for b in range(2)}
-        zeros = keep.tile([P, max(SPARE)], F32, name="zeros")
-        nc.gpsimd.memset(zeros[:], 0.0)
+        early = keep.tile([P, 2, S], BF16, name="early")
+        late_ranges = STEPS[1:]
+        late = [keep.tile([P, 2, hi - lo], BF16, name="late%d" % lo) for lo, hi in late_ranges]
+        res = {}
         for i in range(3):
             for b in range(2):
-                nc.scalar.activation(res[i, b][:, S:], zeros[:, : SPARE[i]], TANH)
+                spare = SPARE if (i, b) == (2, 0) else 0
+                res[i, b] = keep.tile([P, S + spare], F32, name="res%d_%d" % (i, b))
+        zeros = keep.tile([P, SPARE], F32, name="zeros")
+        nc.gpsimd.memset(zeros[:], 0.0)
+        nc.scalar.activation(res[2, 0][:, S:], zeros[:], TANH)
 
-        def weave(step):
-            lo, hi = STEPS[step]
-            woven[step] = shared.tile(
-                [P, 2 * (hi - lo)], U32, name="woven%d" % step, offset=WOVEN_BYTES * lo, align_bytes=64
-            )
-            t = max(t for t, piece in enumerate(PIECES) if piece[0] <= lo)
-            words = picked[t][:, :, lo - PIECES[t][0] : hi - PIECES[t][0]]
-            nc.scalar.copy(out=woven[step][:].rearrange("p (n u) -> p n u", u=2), in_=words.rearrange("p u n -> p n u"))
+        def pick_v(dest, j, lo, hi):
+            nc.vector.tensor_copy(out=dest, in_=rows[j][:].indirect(entries(offs_t, lo, hi)))
+
+        def pick_s(dest, j, lo, hi):
+            nc.scalar.activation(dest, rows[j][:].indirect(entries(offs_t, lo, hi)), COPY)
+
+        def insert(planes, first, lo, hi):
+            nc.vector.tensor_copy(out=x_slots[:, lo:hi, first : first + 2], in_=planes.rearrange("p e n -> p n e"))
 
         def quantise_x(step):
             lo, hi = STEPS[step]
             nc.vector.quantize_mx(
-                out=x_codes[:, lo:hi].bitcast(FP8X4), scales=x_scales[:, lo:hi], in_=woven[step][:].bitcast(BF16)
+                out=x_codes[:, lo:hi].bitcast(FP8X4), scales=x_scales[:, lo:hi], in_=x_bf[:, PACK * lo : PACK * hi]
             )
 
-        def interleave_views(part, tile):
-            w_bf[part] = tile
-            grouped = tile[:].rearrange("p (c n j) -> p c j n", n=4, j=PACK)
-            return grouped, w_raw[part].rearrange("p j (c n) -> p c j n", n=4)
+        w_bf = [
+            keep.tile([P, PACK * P * len(group)], BF16, name="w_bf%d" % g, align_bytes=64)
+            for g, group in enumerate(W_GROUPS)
+        ]
+        w_codes = {}
+        w_scales = {}
 
-        def quantise_w(part, codes):
-            i, lo, hi = W_PARTS[part]
-            scales = keep.tile([P, hi - lo], U8, name="w_scales%d" % part, align_bytes=64)
-            nc.vector.quantize_mx(out=codes[:].bitcast(FP8X4), scales=scales[:], in_=w_bf[part][:])
-            for first in range(lo, hi, P):
-                w_codes[i, first // P] = codes[:, first - lo : first - lo + P]
-                w_scales[i, first // P] = scales[:, first - lo : first - lo + P]
+        def interleave_views(group, place):
+            i, b = W_GROUPS[group][place]
+            dest = w_bf[group][:, PACK * P * place : PACK * P * (place + 1)]
+            grouped = dest.rearrange("p (c n j) -> p c j n", n=4, j=PACK)
+            return grouped, w_raw[i][:, :, b * P : (b + 1) * P].rearrange("p j (c n) -> p c j n", n=4)
 
-        def product(i, b, lo, hi):
-            acc = psum.tile([P, hi - lo], F32, name="acc", tag="ring", bufs=8)
-            nc.tensor.matmul_mx(
-                out=acc[:],
-                lhsT=w_codes[i, b].bitcast(FP8X4),
-                lhsT_scale=w_scales[i, b],
-                rhs=x_codes[:, lo:hi].bitcast(FP8X4),
-                rhs_scale=x_scales[:, lo:hi],
-                start=True,
-                stop=True,
-            )
-            nc.scalar.copy(out=res[i, b][:, lo:hi], in_=acc[:])
+        def quantise_w(group):
+            width = P * len(W_GROUPS[group])
+            codes = keep.tile([P, width], U32, name="w_codes%d" % group, align_bytes=64)
+            scales = keep.tile([P, width], U8, name="w_scales%d" % group, align_bytes=64)
+            nc.vector.quantize_mx(out=codes[:].bitcast(FP8X4), scales=scales[:], in_=w_bf[group][:])
+            for place, block in enumerate(W_GROUPS[group]):
+                w_codes[block] = codes[:, P * place : P * (place + 1)]
+                w_scales[block] = scales[:, P * place : P * (place + 1)]
 
-        def products(i, b):
-            for lo in range(0, S, BANK):
-                product(i, b, lo, lo + BANK)
-
-        def picks(t):
-            return entries(offs_t, *PIECES[t])
-
-        def slot(t, j):
-            return picked[t][:, j // 2, :].bitcast(BF16).rearrange("p (n e) -> p n e", e=2)[:, :, j % 2]
-
-        for j in range(2):
-            cut = (768, 1536)[j]
-            for lo, hi in [(0, 1024), (1024, cut)] if j == 1 else [(0, cut)]:
-                nc.scalar.copy(out=rows_bf[j][:, lo:hi], in_=rows[j][:, lo:hi])
-            nc.vector.tensor_copy(out=rows_bf[j][:, cut:], in_=rows[j][:, cut:])
-            for t in (0,):
-                nc.vector.tensor_copy(out=slot(t, j), in_=rows[j][:].indirect(picks(t)))
-            for t in (1, 2):
-                nc.scalar.activation(slot(t, j), rows_bf[j][:].indirect(picks(t)), COPY)
-            if j == 0:
-                for t in range(len(PIECES)):
-                    nc.vector.tensor_copy(out=slot(t, 2), in_=rows[2][:].indirect(picks(t)))
-
-        nc.scalar.copy(*interleave_views(0, w_bf_first))
-        grouped, planes = interleave_views(1, keep.tile([P, PACK * P], BF16, name="w_bf1", align_bytes=64))
-        nc.gpsimd.tensor_scalar(grouped, planes, 1.0, 0.0, MULT, ADD)
-
-        for piece in range(len(PIECES)):
-            nc.vector.tensor_copy(out=slot(piece, 3), in_=rows[3][:].indirect(picks(piece)))
-        for step in range(len(STEPS)):
-            weave(step)
-        quantise_w(0, keep.tile([P, P], U32, name="w_codes0", align_bytes=64))
-        for step, (lo, hi) in enumerate(STEPS):
-            quantise_x(step)
-            product(0, 0, lo, hi)
-
-        nc.vector.tensor_copy(
-            *interleave_views(2, shared.tile([P, PACK * N], BF16, name="w_bf2", offset=W_BF_AT, align_bytes=64))
-        )
-        quantise_w(1, shared.tile([P, P], U32, name="w_codes1", offset=PICKED_AT, align_bytes=64))
-        quantise_w(2, keep.tile([P, N], U32, name="w_codes2", align_bytes=64))
+        def product(i, b, ranges):
+            first, last = ranges[0][0], ranges[-1][1]
+            acc = psum.tile([P, last - first], F32, name="acc", tag="ring", bufs=8)
+            for lo, hi in ranges:
+                nc.tensor.matmul_mx(
+                    out=acc[:, lo - first : hi - first],
+                    lhsT=w_codes[i, b].bitcast(FP8X4),
+                    lhsT_scale=w_scales[i, b],
+                    rhs=x_codes[:, lo:hi].bitcast(FP8X4),
+                    rhs_scale=x_scales[:, lo:hi],
+                    start=True,
+                    stop=True,
+                )
+            return res[i, b][:, first:last], acc[:]
 
         at_dst = [keep.tile([P, U], F32, name="at_dst%d" % b) for b in range(2)]
         summed = [keep.tile([P, U], F32, name="summed%d" % b) for b in range(2)]
         gate = [keep.tile([P, U], F32, name="gate%d" % b) for b in range(2)]
 
-        def fetch_dst(b):
-            nc.vector.tensor_copy(out=at_dst[b][:], in_=res[0, b][:].indirect(dst_t[:]))
+        def fetch_dst(b, lo, hi):
+            nc.scalar.activation(at_dst[b][:, lo:hi], res[0, b][:].indirect(entries(dst_t, lo, hi)), COPY)
 
-        def add_src(b):
-            nc.vector.tensor_tensor(summed[b][:], res[1, b][:].indirect(src_t[:]), at_dst[b][:], ADD)
+        def add_src(b, lo, hi):
+            nc.vector.tensor_tensor(
+                summed[b][:, lo:hi], res[1, b][:].indirect(entries(src_t, lo, hi)), at_dst[b][:, lo:hi], ADD
+            )
 
-        def squash(b):
-            nc.scalar.activation(gate[b][:], summed[b][:], TANH)
+        def squash(b, lo, hi):
+            nc.scalar.activation(gate[b][:, lo:hi], summed[b][:, lo:hi], TANH)
 
-        def send(b, ranges):
-            for lo, hi in ranges:
-                message = keep.tile([P, hi - lo], F32, name="message%d_%d" % (b, lo))
-                nc.vector.tensor_tensor(message[:], res[2, b][:].indirect(entries(src_t, lo, hi)), gate[b][:, lo:hi], MULT)
-                nc.sync.dma_start(out=out[b * P : (b + 1) * P, lo:hi], in_=message[:])
+        def send(b, lo, hi):
+            message = keep.tile([P, hi - lo], F32, name="message%d_%d" % (b, lo))
+            nc.vector.tensor_tensor(message[:], res[2, b][:].indirect(entries(src_t, lo, hi)), gate[b][:, lo:hi], MULT)
+            nc.sync.dma_start(out=out[b * P : (b + 1) * P, lo:hi], in_=message[:])
 
-        fetch_dst(0)
-        products(0, 1)
-        nc.scalar.copy(
-            *interleave_views(3, shared.tile([P, PACK * N], BF16, name="w_bf3", offset=W_BF_AT, align_bytes=64))
-        )
-        fetch_dst(1)
-        quantise_w(3, keep.tile([P, N], U32, name="w_codes3", align_bytes=64))
-        products(1, 0)
-        add_src(0)
-        products(1, 1)
-        add_src(1)
-        squash(0)
-        products(2, 0)
-        send(0, [(0, U)])
-        products(2, 1)
-        squash(1)
-        send(1, LAST)
+        for j in range(2):
+            pick_v(early[:, j, :384], j, 0, 384)
+            pick_s(early[:, j, 384:], j, 384, S)
+        insert(early[:], 0, 0, S)
+        pick_v(x_slots[:, :DIRECT, 2], 2, 0, DIRECT)
+        for t, (lo, hi) in enumerate(late_ranges):
+            pick_s(late[t][:, 0, :], 2, lo, hi)
+
+        pick_v(x_slots[:, :DIRECT, 3], 3, 0, DIRECT)
+        for t, (lo, hi) in enumerate(late_ranges):
+            pick_s(late[t][:, 1, :], 3, lo, hi)
+        nc.scalar.copy(*interleave_views(0, 0))
+        nc.scalar.copy(*interleave_views(1, 0))
+
+        insert(late[0][:], 2, *late_ranges[0])
+        quantise_x(0)
+        insert(late[1][:], 2, *late_ranges[1])
+        quantise_x(1)
+        insert(late[2][:], 2, *late_ranges[2])
+        quantise_x(2)
+        quantise_w(0)
+        quantise_x(3)
+        quantise_w(1)
+        nc.scalar.copy(*product(0, 0, STEPS[:2]))
+        nc.scalar.copy(*product(0, 0, STEPS[2:]))
+        nc.vector.tensor_copy(*interleave_views(2, 0))
+        nc.vector.tensor_copy(*interleave_views(2, 1))
+        nc.vector.tensor_copy(*product(1, 0, HALVES[:1]))
+        quantise_w(2)
+        nc.vector.tensor_copy(*product(1, 0, HALVES[1:]))
+        for half in HALVES:
+            fetch_dst(0, *half)
+        nc.vector.tensor_copy(*interleave_views(3, 0))
+        nc.vector.tensor_copy(*interleave_views(3, 1))
+        add_src(0, *HALVES[0])
+        quantise_w(3)
+        nc.scalar.copy(*product(2, 0, HALVES[:1]))
+        nc.scalar.copy(*product(2, 0, HALVES[1:]))
+        squash(0, *HALVES[0])
+        add_src(0, *HALVES[1])
+        nc.scalar.copy(*product(0, 1, HALVES[:1]))
+        squash(0, *HALVES[1])
+        nc.scalar.copy(*product(0, 1, HALVES[1:]))
+        nc.scalar.copy(*product(1, 1, HALVES[:1]))
+        for half in HALVES:
+            send(0, *half)
+        fetch_dst(1, *THIRDS[0])
+        nc.vector.tensor_copy(*product(1, 1, HALVES[1:]))
+        fetch_dst(1, *THIRDS[1])
+        add_src(1, *THIRDS[0])
+        nc.scalar.copy(*product(2, 1, HALVES[:1]))
+        fetch_dst(1, *THIRDS[2])
+        add_src(1, *THIRDS[1])
+        nc.scalar.copy(*product(2, 1, HALVES[1:]))
+        squash(1, *THIRDS[0])
+        add_src(1, *THIRDS[2])
+        squash(1, *THIRDS[1])
+        send(1, *LAST[0])
+        squash(1, *THIRDS[2])
+        for lo, hi in LAST[1:]:
+            send(1, lo, hi)

@@ -24,10 +24,11 @@ BANK = 512
 DIRECT = 256
 STEPS = [(0, 256), (256, 512), (512, 768), (768, 1024)]
 HALVES = [(0, 512), (512, 1024)]
-THIRDS = [(0, 384), (384, 768), (768, 1024)]
-LAST = [(0, 384), (384, 768), (768, 896), (896, 1024)]
+LAST = [(512, 896), (896, 1024)]
 SPARE = 16
-W_GROUPS = [[(0, 0)], [(1, 0)], [(2, 0), (0, 1)], [(1, 1), (2, 1)]]
+WHOLE = [(0, 0), (1, 0), (2, 0), (0, 1), (1, 1)]
+W_GROUPS = [[(0, 0)], [(1, 0), (0, 1)], [(1, 1), (2, 0), (2, 1)]]
+FUSED = 512
 
 
 def entries(lst, lo, hi):
@@ -38,6 +39,7 @@ def tile_picked_edgeatt_tanh_e_kernel(tc, xT, w1, w2, w3, offs, src, dst, out):
     nc = tc.nc
     with ExitStack() as ctx:
         keep = ctx.enter_context(tc.tile_pool(name="keep", bufs=1))
+        shared = ctx.enter_context(tc.tile_pool(name="shared", bufs=1))
         psum = ctx.enter_context(tc.psum_pool(name="psum", bufs=1))
 
         offs_t = keep.tile([P, S // LIST_ROWS], U16, name="offs_t")
@@ -67,11 +69,15 @@ def tile_picked_edgeatt_tanh_e_kernel(tc, xT, w1, w2, w3, offs, src, dst, out):
         res = {}
         for i in range(3):
             for b in range(2):
-                spare = SPARE if (i, b) == (2, 0) else 0
-                res[i, b] = keep.tile([P, S + spare], F32, name="res%d_%d" % (i, b))
+                spare = SPARE if (i, b) in WHOLE else 0
+                if (i, b) == (1, 0):
+                    res[i, b] = shared.tile([P, S + spare], F32, name="e0", offset=0)
+                elif (i, b) != (2, 1):
+                    res[i, b] = keep.tile([P, S + spare], F32, name="res%d_%d" % (i, b))
         zeros = keep.tile([P, SPARE], F32, name="zeros")
         nc.gpsimd.memset(zeros[:], 0.0)
-        nc.scalar.activation(res[2, 0][:, S:], zeros[:], TANH)
+        for block in WHOLE:
+            nc.scalar.activation(res[block][:, S:], zeros[:], TANH)
 
         def pick_v(dest, j, lo, hi):
             nc.vector.tensor_copy(out=dest, in_=rows[j][:].indirect(entries(offs_t, lo, hi)))
@@ -82,8 +88,7 @@ def tile_picked_edgeatt_tanh_e_kernel(tc, xT, w1, w2, w3, offs, src, dst, out):
         def insert(planes, first, lo, hi):
             nc.vector.tensor_copy(out=x_slots[:, lo:hi, first : first + 2], in_=planes.rearrange("p e n -> p n e"))
 
-        def quantise_x(step):
-            lo, hi = STEPS[step]
+        def quantise_x(lo, hi):
             nc.vector.quantize_mx(
                 out=x_codes[:, lo:hi].bitcast(FP8X4), scales=x_scales[:, lo:hi], in_=x_bf[:, PACK * lo : PACK * hi]
             )
@@ -110,9 +115,9 @@ def tile_picked_edgeatt_tanh_e_kernel(tc, xT, w1, w2, w3, offs, src, dst, out):
                 w_codes[block] = codes[:, P * place : P * (place + 1)]
                 w_scales[block] = scales[:, P * place : P * (place + 1)]
 
-        def product(i, b, ranges):
+        def product(i, b, ranges, bank):
             first, last = ranges[0][0], ranges[-1][1]
-            acc = psum.tile([P, last - first], F32, name="acc", tag="ring", bufs=8)
+            acc = psum.tile([P, last - first], F32, name="acc", tag="bank%d" % bank)
             for lo, hi in ranges:
                 nc.tensor.matmul_mx(
                     out=acc[:, lo - first : hi - first],
@@ -156,53 +161,46 @@ def tile_picked_edgeatt_tanh_e_kernel(tc, xT, w1, w2, w3, offs, src, dst, out):
         pick_v(x_slots[:, :DIRECT, 3], 3, 0, DIRECT)
         for t, (lo, hi) in enumerate(late_ranges):
             pick_s(late[t][:, 1, :], 3, lo, hi)
-        nc.scalar.copy(*interleave_views(0, 0))
+        nc.scalar.copy(*interleave_views(1, 1))
         nc.scalar.copy(*interleave_views(1, 0))
+        nc.scalar.copy(*interleave_views(2, 0))
 
         insert(late[0][:], 2, *late_ranges[0])
-        quantise_x(0)
+        nc.vector.tensor_copy(*interleave_views(0, 0))
         insert(late[1][:], 2, *late_ranges[1])
-        quantise_x(1)
-        insert(late[2][:], 2, *late_ranges[2])
-        quantise_x(2)
+        quantise_x(*HALVES[0])
         quantise_w(0)
-        quantise_x(3)
+        insert(late[2][:], 2, *late_ranges[2])
+        quantise_x(*STEPS[2])
+        quantise_x(*STEPS[3])
         quantise_w(1)
-        nc.scalar.copy(*product(0, 0, STEPS[:2]))
-        nc.scalar.copy(*product(0, 0, STEPS[2:]))
-        nc.vector.tensor_copy(*interleave_views(2, 0))
+        nc.scalar.copy(*product(0, 0, HALVES[:1], 0))
+        nc.scalar.copy(*product(0, 0, STEPS[2:], 1))
         nc.vector.tensor_copy(*interleave_views(2, 1))
-        nc.vector.tensor_copy(*product(1, 0, HALVES[:1]))
+        nc.vector.tensor_copy(*interleave_views(2, 2))
+        nc.vector.tensor_copy(*product(1, 0, HALVES[:1], 2))
         quantise_w(2)
-        nc.vector.tensor_copy(*product(1, 0, HALVES[1:]))
-        for half in HALVES:
-            fetch_dst(0, *half)
-        nc.vector.tensor_copy(*interleave_views(3, 0))
-        nc.vector.tensor_copy(*interleave_views(3, 1))
-        add_src(0, *HALVES[0])
-        quantise_w(3)
-        nc.scalar.copy(*product(2, 0, HALVES[:1]))
-        nc.scalar.copy(*product(2, 0, HALVES[1:]))
-        squash(0, *HALVES[0])
-        add_src(0, *HALVES[1])
-        nc.scalar.copy(*product(0, 1, HALVES[:1]))
-        squash(0, *HALVES[1])
-        nc.scalar.copy(*product(0, 1, HALVES[1:]))
-        nc.scalar.copy(*product(1, 1, HALVES[:1]))
-        for half in HALVES:
-            send(0, *half)
-        fetch_dst(1, *THIRDS[0])
-        nc.vector.tensor_copy(*product(1, 1, HALVES[1:]))
-        fetch_dst(1, *THIRDS[1])
-        add_src(1, *THIRDS[0])
-        nc.scalar.copy(*product(2, 1, HALVES[:1]))
-        fetch_dst(1, *THIRDS[2])
-        add_src(1, *THIRDS[1])
-        nc.scalar.copy(*product(2, 1, HALVES[1:]))
-        squash(1, *THIRDS[0])
-        add_src(1, *THIRDS[2])
-        squash(1, *THIRDS[1])
-        send(1, *LAST[0])
-        squash(1, *THIRDS[2])
-        for lo, hi in LAST[1:]:
-            send(1, lo, hi)
+        nc.vector.tensor_copy(*product(1, 0, HALVES[1:], 5))
+        fetch_dst(0, 0, U)
+        nc.vector.tensor_copy(*product(0, 1, HALVES[:1], 3))
+        nc.vector.tensor_copy(*product(0, 1, HALVES[1:], 4))
+        nc.scalar.copy(*product(1, 1, HALVES[:1], 6))
+        nc.vector.tensor_copy(*product(1, 1, HALVES[1:], 7))
+        fetch_dst(1, 0, U)
+        add_src(0, 0, U)
+        add_src(1, 0, U)
+        nc.scalar.copy(*product(2, 0, HALVES[:1], 4))
+        nc.scalar.copy(*product(2, 0, HALVES[1:], 7))
+        squash(0, 0, U)
+        send(0, 0, U)
+        res[2, 1] = shared.tile([P, S], F32, name="h1", offset=0)
+        nc.scalar.copy(*product(2, 1, HALVES[:1], 0))
+        nc.scalar.copy(*product(2, 1, HALVES[1:], 1))
+        squash(1, 0, U)
+        send(1, 0, FUSED)
+        at_src = keep.tile([P, U - FUSED], F32, name="at_src")
+        nc.scalar.activation(at_src[:], res[2, 1][:].indirect(entries(src_t, FUSED, U)), COPY)
+        for lo, hi in LAST:
+            message = keep.tile([P, hi - lo], F32, name="message1_%d" % lo)
+            nc.vector.tensor_tensor(message[:], at_src[:, lo - FUSED : hi - FUSED], gate[1][:, lo:hi], MULT)
+            nc.sync.dma_start(out=out[P:, lo:hi], in_=message[:])

@@ -29,6 +29,7 @@ SPARE = 16
 WHOLE = [(0, 0), (1, 0), (2, 0), (0, 1), (1, 1)]
 W_GROUPS = [[(0, 0)], [(1, 0), (0, 1)], [(1, 1), (2, 0), (2, 1)]]
 FUSED = 512
+W_LOADS = [(0, 0, 128), (0, 128, 256), (1, 0, 256), (2, 0, 256)]
 
 
 def entries(lst, lo, hi):
@@ -52,10 +53,12 @@ def tile_picked_edgeatt_tanh_e_kernel(tc, xT, w1, w2, w3, offs, src, dst, out):
             nc.sync.dma_start(out=rows[j][:], in_=x_rows[:, j, :])
             if j == 0:
                 nc.sync.dma_start(offs_t[:], offs)
-        w_raw = []
-        for i, w in enumerate((w1, w2, w3)):
-            w_raw.append(keep.tile([P, PACK, N], F32, name="w_raw%d" % i))
-            nc.sync.dma_start(out=w_raw[i][:], in_=w.rearrange("(p j) n -> p j n", j=PACK))
+        w_raw = {}
+        for i, lo, hi in W_LOADS:
+            raw = keep.tile([P, PACK, hi - lo], F32, name="w_raw%d_%d" % (i, lo))
+            nc.sync.dma_start(out=raw[:], in_=(w1, w2, w3)[i].rearrange("(p j) n -> p j n", j=PACK)[:, :, lo:hi])
+            for b in range(lo // P, hi // P):
+                w_raw[i, b] = (raw, b * P - lo)
         nc.sync.dma_start(dst_t[:], dst)
         nc.sync.dma_start(src_t[:], src)
 
@@ -100,11 +103,11 @@ def tile_picked_edgeatt_tanh_e_kernel(tc, xT, w1, w2, w3, offs, src, dst, out):
         w_codes = {}
         w_scales = {}
 
-        def interleave_views(group, place):
-            i, b = W_GROUPS[group][place]
-            dest = w_bf[group][:, PACK * P * place : PACK * P * (place + 1)]
+        def interleave_views(group, place, blocks=1):
+            raw, first = w_raw[W_GROUPS[group][place]]
+            dest = w_bf[group][:, PACK * P * place : PACK * P * (place + blocks)]
             grouped = dest.rearrange("p (c n j) -> p c j n", n=4, j=PACK)
-            return grouped, w_raw[i][:, :, b * P : (b + 1) * P].rearrange("p j (c n) -> p c j n", n=4)
+            return grouped, raw[:, :, first : first + blocks * P].rearrange("p j (c n) -> p c j n", n=4)
 
         def quantise_w(group):
             width = P * len(W_GROUPS[group])
@@ -151,8 +154,8 @@ def tile_picked_edgeatt_tanh_e_kernel(tc, xT, w1, w2, w3, offs, src, dst, out):
             nc.sync.dma_start(out=out[b * P : (b + 1) * P, lo:hi], in_=message[:])
 
         for j in range(2):
-            pick_v(early[:, j, :384], j, 0, 384)
-            pick_s(early[:, j, 384:], j, 384, S)
+            pick_v(early[:, j, :512], j, 0, 512)
+            pick_s(early[:, j, 512:], j, 512, S)
         insert(early[:], 0, 0, S)
         pick_v(x_slots[:, :DIRECT, 2], 2, 0, DIRECT)
         for t, (lo, hi) in enumerate(late_ranges):
@@ -165,19 +168,18 @@ def tile_picked_edgeatt_tanh_e_kernel(tc, xT, w1, w2, w3, offs, src, dst, out):
         nc.scalar.copy(*interleave_views(1, 0))
         nc.scalar.copy(*interleave_views(2, 0))
 
-        insert(late[0][:], 2, *late_ranges[0])
         nc.vector.tensor_copy(*interleave_views(0, 0))
+        insert(late[0][:], 2, *late_ranges[0])
         insert(late[1][:], 2, *late_ranges[1])
-        quantise_x(*HALVES[0])
         quantise_w(0)
+        quantise_x(*HALVES[0])
         insert(late[2][:], 2, *late_ranges[2])
         quantise_x(*STEPS[2])
         quantise_x(*STEPS[3])
         quantise_w(1)
         nc.scalar.copy(*product(0, 0, HALVES[:1], 0))
         nc.scalar.copy(*product(0, 0, STEPS[2:], 1))
-        nc.vector.tensor_copy(*interleave_views(2, 1))
-        nc.vector.tensor_copy(*interleave_views(2, 2))
+        nc.vector.tensor_copy(*interleave_views(2, 1, 2))
         nc.vector.tensor_copy(*product(1, 0, HALVES[:1], 2))
         quantise_w(2)
         nc.vector.tensor_copy(*product(1, 0, HALVES[1:], 5))

@@ -24,11 +24,10 @@ BANK = 512
 DIRECT = 256
 STEPS = [(0, 256), (256, 512), (512, 768), (768, 1024)]
 HALVES = [(0, 512), (512, 1024)]
-LAST = [(512, 896), (896, 1024)]
 SPARE = 16
 WHOLE = [(0, 0), (1, 0), (2, 0), (0, 1), (1, 1)]
 W_GROUPS = [[(0, 0)], [(1, 0), (0, 1)], [(1, 1), (2, 0), (2, 1)]]
-FUSED = 512
+PLAIN = (512, 896)
 W_LOADS = [(0, 0, 128), (0, 128, 256), (1, 0, 256), (2, 0, 256)]
 
 
@@ -68,7 +67,8 @@ def tile_picked_edgeatt_tanh_e_kernel(tc, xT, w1, w2, w3, offs, src, dst, out):
         x_scales = keep.tile([P, S], U8, name="x_scales", align_bytes=64)
         early = keep.tile([P, 2, S], BF16, name="early")
         late_ranges = STEPS[1:]
-        late = [keep.tile([P, 2, hi - lo], BF16, name="late%d" % lo) for lo, hi in late_ranges]
+        late = keep.tile([P, 2 * (S - DIRECT)], BF16, name="late")
+        late_planes = late[:].rearrange("p (e n) -> p e n", e=2)
         res = {}
         for i in range(3):
             for b in range(2):
@@ -90,6 +90,9 @@ def tile_picked_edgeatt_tanh_e_kernel(tc, xT, w1, w2, w3, offs, src, dst, out):
 
         def insert(planes, first, lo, hi):
             nc.vector.tensor_copy(out=x_slots[:, lo:hi, first : first + 2], in_=planes.rearrange("p e n -> p n e"))
+
+        def insert_late(lo, hi):
+            insert(late_planes[:, :, lo - DIRECT : hi - DIRECT], 2, lo, hi)
 
         def quantise_x(lo, hi):
             nc.vector.quantize_mx(
@@ -158,22 +161,21 @@ def tile_picked_edgeatt_tanh_e_kernel(tc, xT, w1, w2, w3, offs, src, dst, out):
             pick_s(early[:, j, 512:], j, 512, S)
         insert(early[:], 0, 0, S)
         pick_v(x_slots[:, :DIRECT, 2], 2, 0, DIRECT)
-        for t, (lo, hi) in enumerate(late_ranges):
-            pick_s(late[t][:, 0, :], 2, lo, hi)
+        pick_s(late_planes[:, 0, :], 2, DIRECT, S)
 
         pick_v(x_slots[:, :DIRECT, 3], 3, 0, DIRECT)
-        for t, (lo, hi) in enumerate(late_ranges):
-            pick_s(late[t][:, 1, :], 3, lo, hi)
+        for lo, hi in late_ranges:
+            pick_s(late_planes[:, 1, lo - DIRECT : hi - DIRECT], 3, lo, hi)
         nc.scalar.copy(*interleave_views(1, 1))
         nc.scalar.copy(*interleave_views(1, 0))
         nc.scalar.copy(*interleave_views(2, 0))
 
         nc.vector.tensor_copy(*interleave_views(0, 0))
-        insert(late[0][:], 2, *late_ranges[0])
-        insert(late[1][:], 2, *late_ranges[1])
+        insert_late(*late_ranges[0])
+        insert_late(*late_ranges[1])
         quantise_w(0)
         quantise_x(*HALVES[0])
-        insert(late[2][:], 2, *late_ranges[2])
+        insert_late(*late_ranges[2])
         quantise_x(*STEPS[2])
         quantise_x(*STEPS[3])
         quantise_w(1)
@@ -199,10 +201,11 @@ def tile_picked_edgeatt_tanh_e_kernel(tc, xT, w1, w2, w3, offs, src, dst, out):
         nc.scalar.copy(*product(2, 1, HALVES[:1], 0))
         nc.scalar.copy(*product(2, 1, HALVES[1:], 1))
         squash(1, 0, U)
-        send(1, 0, FUSED)
-        at_src = keep.tile([P, U - FUSED], F32, name="at_src")
-        nc.scalar.activation(at_src[:], res[2, 1][:].indirect(entries(src_t, FUSED, U)), COPY)
-        for lo, hi in LAST:
-            message = keep.tile([P, hi - lo], F32, name="message1_%d" % lo)
-            nc.vector.tensor_tensor(message[:], at_src[:, lo - FUSED : hi - FUSED], gate[1][:, lo:hi], MULT)
-            nc.sync.dma_start(out=out[P:, lo:hi], in_=message[:])
+        lo, hi = PLAIN
+        send(1, 0, lo)
+        at_src = keep.tile([P, hi - lo], F32, name="at_src")
+        nc.scalar.activation(at_src[:], res[2, 1][:].indirect(entries(src_t, lo, hi)), COPY)
+        message = keep.tile([P, hi - lo], F32, name="plain_message")
+        nc.vector.tensor_tensor(message[:], at_src[:], gate[1][:, lo:hi], MULT)
+        nc.sync.dma_start(out=out[P:, lo:hi], in_=message[:])
+        send(1, hi, U)

@@ -25,8 +25,9 @@ DIRECT = 256
 STEPS = [(0, 256), (256, 512), (512, 768), (768, 1024)]
 HALVES = [(0, 512), (512, 1024)]
 SPARE = 16
+COPY_SPARE = 352
 WHOLE = [(0, 0), (1, 0), (2, 0), (0, 1), (1, 1)]
-W_GROUPS = [[(0, 0)], [(1, 0), (0, 1)], [(1, 1), (2, 0), (2, 1)]]
+W_GROUPS = [[(0, 0)], [(1, 0), (0, 1)], [(1, 1)], [(2, 0), (2, 1)]]
 PLAIN = (512, 896)
 W_LOADS = [(0, 0, 128), (0, 128, 256), (1, 0, 256), (2, 0, 256)]
 
@@ -72,15 +73,15 @@ def tile_picked_edgeatt_tanh_e_kernel(tc, xT, w1, w2, w3, offs, src, dst, out):
         res = {}
         for i in range(3):
             for b in range(2):
-                spare = SPARE if (i, b) in WHOLE else 0
+                spare = (COPY_SPARE if (i, b) == (0, 0) else SPARE) if (i, b) in WHOLE else 0
                 if (i, b) == (1, 0):
                     res[i, b] = shared.tile([P, S + spare], F32, name="e0", offset=0)
                 elif (i, b) != (2, 1):
                     res[i, b] = keep.tile([P, S + spare], F32, name="res%d_%d" % (i, b))
-        zeros = keep.tile([P, SPARE], F32, name="zeros")
+        zeros = keep.tile([P, COPY_SPARE], F32, name="zeros")
         nc.gpsimd.memset(zeros[:], 0.0)
         for block in WHOLE:
-            nc.scalar.activation(res[block][:, S:], zeros[:], TANH)
+            nc.scalar.activation(res[block][:, S:], zeros[:, : res[block].shape[1] - S], TANH)
 
         def pick_v(dest, j, lo, hi):
             nc.vector.tensor_copy(out=dest, in_=rows[j][:].indirect(entries(offs_t, lo, hi)))
@@ -181,20 +182,21 @@ def tile_picked_edgeatt_tanh_e_kernel(tc, xT, w1, w2, w3, offs, src, dst, out):
         quantise_w(1)
         nc.scalar.copy(*product(0, 0, HALVES[:1], 0))
         nc.scalar.copy(*product(0, 0, STEPS[2:], 1))
-        nc.vector.tensor_copy(*interleave_views(2, 1, 2))
-        nc.vector.tensor_copy(*product(1, 0, HALVES[:1], 2))
+        nc.vector.tensor_copy(*interleave_views(3, 0, 2))
         quantise_w(2)
-        nc.vector.tensor_copy(*product(1, 0, HALVES[1:], 5))
-        fetch_dst(0, 0, U)
-        nc.vector.tensor_copy(*product(0, 1, HALVES[:1], 3))
-        nc.vector.tensor_copy(*product(0, 1, HALVES[1:], 4))
+        quantise_w(3)
+        nc.vector.tensor_copy(out=at_dst[0][:], in_=res[0, 0][:].indirect(dst_t[:]))
+        nc.scalar.copy(*product(1, 0, HALVES[:1], 2))
+        nc.scalar.copy(*product(1, 0, HALVES[1:], 5))
+        nc.scalar.copy(*product(0, 1, HALVES[:1], 3))
+        nc.scalar.copy(*product(0, 1, HALVES[1:], 4))
         nc.scalar.copy(*product(1, 1, HALVES[:1], 6))
-        nc.vector.tensor_copy(*product(1, 1, HALVES[1:], 7))
+        nc.vector.tensor_copy(*product(1, 1, HALVES[1:], 2))
         fetch_dst(1, 0, U)
         add_src(0, 0, U)
         add_src(1, 0, U)
-        nc.scalar.copy(*product(2, 0, HALVES[:1], 4))
-        nc.scalar.copy(*product(2, 0, HALVES[1:], 7))
+        nc.scalar.copy(*product(2, 0, HALVES[:1], 6))
+        nc.scalar.copy(*product(2, 0, HALVES[1:], 6))
         squash(0, 0, U)
         send(0, 0, U)
         res[2, 1] = shared.tile([P, S], F32, name="h1", offset=0)

@@ -26,7 +26,7 @@ STEPS = [(0, 256), (256, 512), (512, 768), (768, 1024)]
 HALVES = [(0, 512), (512, 1024)]
 SPARE = 16
 COPY_SPARE = 352
-WHOLE = [(0, 0), (1, 0), (2, 0), (0, 1), (1, 1)]
+WHOLE = [(0, 0), (1, 0), (0, 1), (1, 1)]
 W_GROUPS = [[(0, 0)], [(1, 0), (0, 1)], [(1, 1)], [(2, 0), (2, 1)]]
 PLAIN = (512, 896)
 W_LOADS = [(0, 0, 128), (0, 128, 256), (1, 0, 256), (2, 0, 256)]
@@ -197,8 +197,9 @@ def tile_picked_edgeatt_tanh_e_kernel(tc, xT, w1, w2, w3, offs, src, dst, out):
         add_src(1, 0, U)
         nc.scalar.copy(*product(2, 0, HALVES[:1], 6))
         nc.scalar.copy(*product(2, 0, HALVES[1:], 6))
-        squash(0, 0, U)
-        send(0, 0, U)
+        for half in HALVES:
+            squash(0, *half)
+            send(0, *half)
         res[2, 1] = shared.tile([P, S], F32, name="h1", offset=0)
         nc.scalar.copy(*product(2, 1, HALVES[:1], 0))
         nc.scalar.copy(*product(2, 1, HALVES[1:], 1))

@@ -19,17 +19,14 @@ COPY = mybir.ActivationFunctionType.Copy
 P = 128
 PACK = 4
 LIST_ROWS = 16
-BANK = 512
+Y, E, H = 0, 1, 2
 
 DIRECT = 256
 STEPS = [(0, 256), (256, 512), (512, 768), (768, 1024)]
 HALVES = [(0, 512), (512, 1024)]
-SPARE = 16
-COPY_SPARE = 352
-WHOLE = [(0, 0), (1, 0), (0, 1), (1, 1)]
-W_GROUPS = [[(0, 0)], [(1, 0), (0, 1)], [(1, 1)], [(2, 0), (2, 1)]]
+E_SPARE = 16
 PLAIN = (512, 896)
-W_LOADS = [(0, 0, 128), (0, 128, 256), (1, 0, 256), (2, 0, 256)]
+W_LOADS = [(Y, 0, 128), (Y, 128, 256), (E, 0, 128), (E, 128, 256), (H, 0, 256)]
 
 
 def entries(lst, lo, hi):
@@ -40,7 +37,8 @@ def tile_picked_edgeatt_tanh_e_kernel(tc, xT, w1, w2, w3, offs, src, dst, out):
     nc = tc.nc
     with ExitStack() as ctx:
         keep = ctx.enter_context(tc.tile_pool(name="keep", bufs=1))
-        shared = ctx.enter_context(tc.tile_pool(name="shared", bufs=1))
+        chain = ctx.enter_context(tc.tile_pool(name="chain", bufs=1))
+        reuse = ctx.enter_context(tc.tile_pool(name="reuse", bufs=1))
         psum = ctx.enter_context(tc.psum_pool(name="psum", bufs=1))
 
         offs_t = keep.tile([P, S // LIST_ROWS], U16, name="offs_t")
@@ -55,7 +53,10 @@ def tile_picked_edgeatt_tanh_e_kernel(tc, xT, w1, w2, w3, offs, src, dst, out):
                 nc.sync.dma_start(offs_t[:], offs)
         w_raw = {}
         for i, lo, hi in W_LOADS:
-            raw = keep.tile([P, PACK, hi - lo], F32, name="w_raw%d_%d" % (i, lo))
+            if (i, lo) == (E, 0):
+                raw = reuse.tile([P, PACK, hi - lo], F32, name="we0_raw", offset=20480, align_bytes=64)
+            else:
+                raw = keep.tile([P, PACK, hi - lo], F32, name="w_raw%d_%d" % (i, lo))
             nc.sync.dma_start(out=raw[:], in_=(w1, w2, w3)[i].rearrange("(p j) n -> p j n", j=PACK)[:, :, lo:hi])
             for b in range(lo // P, hi // P):
                 w_raw[i, b] = (raw, b * P - lo)
@@ -67,21 +68,15 @@ def tile_picked_edgeatt_tanh_e_kernel(tc, xT, w1, w2, w3, offs, src, dst, out):
         x_codes = keep.tile([P, S], U32, name="x_codes", align_bytes=64)
         x_scales = keep.tile([P, S], U8, name="x_scales", align_bytes=64)
         early = keep.tile([P, 2, S], BF16, name="early")
-        late_ranges = STEPS[1:]
         late = keep.tile([P, 2 * (S - DIRECT)], BF16, name="late")
         late_planes = late[:].rearrange("p (e n) -> p e n", e=2)
+
         res = {}
-        for i in range(3):
-            for b in range(2):
-                spare = (COPY_SPARE if (i, b) == (0, 0) else SPARE) if (i, b) in WHOLE else 0
-                if (i, b) == (1, 0):
-                    res[i, b] = shared.tile([P, S + spare], F32, name="e0", offset=0)
-                elif (i, b) != (2, 1):
-                    res[i, b] = keep.tile([P, S + spare], F32, name="res%d_%d" % (i, b))
-        zeros = keep.tile([P, COPY_SPARE], F32, name="zeros")
+        res[E, 0] = reuse.tile([P, S + E_SPARE], F32, name="e0", offset=0, align_bytes=64)
+        res[Y, 1] = reuse.tile([P, S], F32, name="y1", offset=8192, align_bytes=64)
+        zeros = keep.tile([P, E_SPARE], F32, name="zeros")
         nc.gpsimd.memset(zeros[:], 0.0)
-        for block in WHOLE:
-            nc.scalar.activation(res[block][:, S:], zeros[:, : res[block].shape[1] - S], TANH)
+        nc.scalar.activation(res[E, 0][:, S:], zeros[:], TANH)
 
         def pick_v(dest, j, lo, hi):
             nc.vector.tensor_copy(out=dest, in_=rows[j][:].indirect(entries(offs_t, lo, hi)))
@@ -100,32 +95,38 @@ def tile_picked_edgeatt_tanh_e_kernel(tc, xT, w1, w2, w3, offs, src, dst, out):
                 out=x_codes[:, lo:hi].bitcast(FP8X4), scales=x_scales[:, lo:hi], in_=x_bf[:, PACK * lo : PACK * hi]
             )
 
-        w_bf = [
-            keep.tile([P, PACK * P * len(group)], BF16, name="w_bf%d" % g, align_bytes=64)
-            for g, group in enumerate(W_GROUPS)
-        ]
         w_codes = {}
         w_scales = {}
 
-        def interleave_views(group, place, blocks=1):
-            raw, first = w_raw[W_GROUPS[group][place]]
-            dest = w_bf[group][:, PACK * P * place : PACK * P * (place + blocks)]
+        def grouped_views(dest, i, b):
             grouped = dest.rearrange("p (c n j) -> p c j n", n=4, j=PACK)
-            return grouped, raw[:, :, first : first + blocks * P].rearrange("p j (c n) -> p c j n", n=4)
+            raw, first = w_raw[i, b]
+            return grouped, raw[:, :, first : first + P].rearrange("p j (c n) -> p c j n", n=4)
 
-        def quantise_w(group):
-            width = P * len(W_GROUPS[group])
-            codes = keep.tile([P, width], U32, name="w_codes%d" % group, align_bytes=64)
-            scales = keep.tile([P, width], U8, name="w_scales%d" % group, align_bytes=64)
-            nc.vector.quantize_mx(out=codes[:].bitcast(FP8X4), scales=scales[:], in_=w_bf[group][:])
-            for place, block in enumerate(W_GROUPS[group]):
+        def interleave_gpsimd(dest, i, b):
+            nc.gpsimd.tensor_scalar(
+                dest[:].rearrange("p (n j) -> p n j", j=PACK),
+                w_raw[i, b][0][:].rearrange("p j n -> p n j"),
+                1.0,
+                0.0,
+                MULT,
+                ADD,
+            )
+
+        def quantise_w(source, blocks, codes=None):
+            width = P * len(blocks)
+            if codes is None:
+                codes = keep.tile([P, width], U32, name="w_codes%d_%d" % blocks[0], align_bytes=64)
+            scales = keep.tile([P, width], U8, name="w_scales%d_%d" % blocks[0], align_bytes=64)
+            nc.vector.quantize_mx(out=codes[:].bitcast(FP8X4), scales=scales[:], in_=source[:])
+            for place, block in enumerate(blocks):
                 w_codes[block] = codes[:, P * place : P * (place + 1)]
                 w_scales[block] = scales[:, P * place : P * (place + 1)]
 
-        def product(i, b, ranges, bank):
-            first, last = ranges[0][0], ranges[-1][1]
+        def product(i, b, first, last, bank, width=512):
             acc = psum.tile([P, last - first], F32, name="acc", tag="bank%d" % bank)
-            for lo, hi in ranges:
+            for lo in range(first, last, width):
+                hi = min(lo + width, last)
                 nc.tensor.matmul_mx(
                     out=acc[:, lo - first : hi - first],
                     lhsT=w_codes[i, b].bitcast(FP8X4),
@@ -135,26 +136,11 @@ def tile_picked_edgeatt_tanh_e_kernel(tc, xT, w1, w2, w3, offs, src, dst, out):
                     start=True,
                     stop=True,
                 )
-            return res[i, b][:, first:last], acc[:]
+            nc.scalar.copy(res[i, b][:, first:last], acc[:])
 
-        at_dst = [keep.tile([P, U], F32, name="at_dst%d" % b) for b in range(2)]
-        summed = [keep.tile([P, U], F32, name="summed%d" % b) for b in range(2)]
-        gate = [keep.tile([P, U], F32, name="gate%d" % b) for b in range(2)]
-
-        def fetch_dst(b, lo, hi):
-            nc.scalar.activation(at_dst[b][:, lo:hi], res[0, b][:].indirect(entries(dst_t, lo, hi)), COPY)
-
-        def add_src(b, lo, hi):
-            nc.vector.tensor_tensor(
-                summed[b][:, lo:hi], res[1, b][:].indirect(entries(src_t, lo, hi)), at_dst[b][:, lo:hi], ADD
-            )
-
-        def squash(b, lo, hi):
-            nc.scalar.activation(gate[b][:, lo:hi], summed[b][:, lo:hi], TANH)
-
-        def send(b, lo, hi):
+        def send(b, gate, lo, hi):
             message = keep.tile([P, hi - lo], F32, name="message%d_%d" % (b, lo))
-            nc.vector.tensor_tensor(message[:], res[2, b][:].indirect(entries(src_t, lo, hi)), gate[b][:, lo:hi], MULT)
+            nc.vector.tensor_tensor(message[:], res[H, b][:].indirect(entries(src_t, lo, hi)), gate[:, lo:hi], MULT)
             nc.sync.dma_start(out=out[b * P : (b + 1) * P, lo:hi], in_=message[:])
 
         for j in range(2):
@@ -165,50 +151,88 @@ def tile_picked_edgeatt_tanh_e_kernel(tc, xT, w1, w2, w3, offs, src, dst, out):
         pick_s(late_planes[:, 0, :], 2, DIRECT, S)
 
         pick_v(x_slots[:, :DIRECT, 3], 3, 0, DIRECT)
-        for lo, hi in late_ranges:
+        for lo, hi in STEPS[1:]:
             pick_s(late_planes[:, 1, lo - DIRECT : hi - DIRECT], 3, lo, hi)
-        nc.scalar.copy(*interleave_views(1, 1))
-        nc.scalar.copy(*interleave_views(1, 0))
-        nc.scalar.copy(*interleave_views(2, 0))
+        first_bf = keep.tile([P, PACK * P], BF16, name="first_bf", align_bytes=64)
+        second_bf = chain.tile([P, 2 * PACK * P], BF16, name="second_bf", offset=2560, align_bytes=64)
+        nc.scalar.copy(*grouped_views(second_bf[:, : PACK * P], Y, 1))
+        nc.scalar.copy(*grouped_views(second_bf[:, PACK * P :], E, 0))
 
-        nc.vector.tensor_copy(*interleave_views(0, 0))
-        insert_late(*late_ranges[0])
-        insert_late(*late_ranges[1])
-        quantise_w(0)
-        quantise_x(*HALVES[0])
-        insert_late(*late_ranges[2])
+        insert_late(*STEPS[1])
+        nc.vector.tensor_copy(*grouped_views(first_bf[:], Y, 0))
+        quantise_x(*STEPS[0])
+        quantise_w(first_bf, [(Y, 0)])
+        insert_late(*STEPS[2])
+        quantise_x(*STEPS[1])
+        insert_late(*STEPS[3])
         quantise_x(*STEPS[2])
         quantise_x(*STEPS[3])
-        quantise_w(1)
-        nc.scalar.copy(*product(0, 0, HALVES[:1], 0))
-        nc.scalar.copy(*product(0, 0, STEPS[2:], 1))
-        nc.vector.tensor_copy(*interleave_views(3, 0, 2))
-        quantise_w(2)
-        quantise_w(3)
-        nc.vector.tensor_copy(out=at_dst[0][:], in_=res[0, 0][:].indirect(dst_t[:]))
-        nc.scalar.copy(*product(1, 0, HALVES[:1], 2))
-        nc.scalar.copy(*product(1, 0, HALVES[1:], 5))
-        nc.scalar.copy(*product(0, 1, HALVES[:1], 3))
-        nc.scalar.copy(*product(0, 1, HALVES[1:], 4))
-        nc.scalar.copy(*product(1, 1, HALVES[:1], 6))
-        nc.vector.tensor_copy(*product(1, 1, HALVES[1:], 2))
-        fetch_dst(1, 0, U)
-        add_src(0, 0, U)
-        add_src(1, 0, U)
-        nc.scalar.copy(*product(2, 0, HALVES[:1], 6))
-        nc.scalar.copy(*product(2, 0, HALVES[1:], 6))
-        for half in HALVES:
-            squash(0, *half)
-            send(0, *half)
-        res[2, 1] = shared.tile([P, S], F32, name="h1", offset=0)
-        nc.scalar.copy(*product(2, 1, HALVES[:1], 0))
-        nc.scalar.copy(*product(2, 1, HALVES[1:], 1))
-        squash(1, 0, U)
+        quantise_w(second_bf, [(Y, 1), (E, 0)])
+        we1_bf = chain.tile([P, PACK * P], BF16, name="we1_bf", offset=2560, align_bytes=64)
+        nc.vector.tensor_copy(*grouped_views(we1_bf[:], E, 1))
+        quantise_w(we1_bf, [(E, 1)])
+
+        res[Y, 0] = reuse.tile([P, S], F32, name="y0", offset=20480, align_bytes=64)
+        product(Y, 0, *HALVES[0], 0, 256)
+        product(Y, 0, *STEPS[2], 1)
+        product(Y, 0, *STEPS[3], 2)
+        at_dst0 = keep.tile([P, U], F32, name="at_dst0")
+        for lo, hi in HALVES:
+            nc.vector.tensor_copy(out=at_dst0[:, lo:hi], in_=res[Y, 0][:].indirect(entries(dst_t, lo, hi)))
+
+        wh_bf = chain.tile([P, PACK * N], BF16, name="wh_bf", offset=3328, align_bytes=64)
+        interleave_gpsimd(wh_bf, H, 0)
+        quantise_w(wh_bf, [(H, 0), (H, 1)])
+
+        product(Y, 1, *HALVES[0], 3)
+        product(Y, 1, *HALVES[1], 4)
+        product(E, 0, *HALVES[0], 5)
+        product(E, 0, *HALVES[1], 6)
+        summed0 = chain.tile([P, U], F32, name="summed0", offset=5120, align_bytes=64)
+        nc.vector.tensor_tensor(summed0[:], res[E, 0][:].indirect(src_t[:]), at_dst0[:], ADD)
+
+        res[E, 1] = keep.tile([P, S], F32, name="e1")
+        summed1 = chain.tile([P, U], F32, name="summed1", offset=0, align_bytes=64)
+        at_dst1 = [
+            keep.tile([P, 512], F32, name="at_dst1a"),
+            keep.tile([P, 512], F32, name="at_dst1b"),
+        ]
+
+        def fetch_dst1(half):
+            nc.scalar.activation(at_dst1[half][:], res[Y, 1][:].indirect(entries(dst_t, *HALVES[half])), COPY)
+
+        def add_src1(half):
+            lo, hi = HALVES[half]
+            nc.vector.tensor_tensor(
+                summed1[:, lo:hi], res[E, 1][:].indirect(entries(src_t, lo, hi)), at_dst1[half][:], ADD
+            )
+
+        product(E, 1, *HALVES[0], 7)
+        product(E, 1, *HALVES[1], 0)
+        fetch_dst1(0)
+        fetch_dst1(1)
+        add_src1(0)
+        add_src1(1)
+
+        res[H, 0] = keep.tile([P, S], F32, name="h0")
+        product(H, 0, *HALVES[0], 7)
+        product(H, 0, *HALVES[1], 0)
+        gate0 = reuse.tile([P, U], F32, name="gate0", offset=8192, align_bytes=64)
+        for lo, hi in HALVES:
+            nc.scalar.activation(gate0[:, lo:hi], summed0[:, lo:hi], TANH)
+            send(0, gate0, lo, hi)
+
+        res[H, 1] = reuse.tile([P, S], F32, name="h1", offset=0, align_bytes=64)
+        product(H, 1, *HALVES[0], 1)
+        product(H, 1, *HALVES[1], 2)
+        gate1 = keep.tile([P, U], F32, name="gate1")
+        for lo, hi in HALVES:
+            nc.scalar.activation(gate1[:, lo:hi], summed1[:, lo:hi], TANH)
         lo, hi = PLAIN
-        send(1, 0, lo)
+        send(1, gate1, 0, lo)
         at_src = keep.tile([P, hi - lo], F32, name="at_src")
-        nc.scalar.activation(at_src[:], res[2, 1][:].indirect(entries(src_t, lo, hi)), COPY)
+        nc.scalar.activation(at_src[:], res[H, 1][:].indirect(entries(src_t, lo, hi)), COPY)
         message = keep.tile([P, hi - lo], F32, name="plain_message")
-        nc.vector.tensor_tensor(message[:], at_src[:], gate[1][:, lo:hi], MULT)
+        nc.vector.tensor_tensor(message[:], at_src[:], gate1[:, lo:hi], MULT)
         nc.sync.dma_start(out=out[P:, lo:hi], in_=message[:])
-        send(1, hi, U)
+        send(1, gate1, hi, U)

@@ -24,9 +24,10 @@ Y, E, H = 0, 1, 2
 DIRECT = 256
 STEPS = [(0, 256), (256, 512), (512, 768), (768, 1024)]
 HALVES = [(0, 512), (512, 1024)]
-E_SPARE = 16
-PLAIN = (512, 896)
-W_LOADS = [(Y, 0, 128), (Y, 128, 256), (E, 0, 128), (E, 128, 256), (H, 0, 256)]
+COPY_SPARE = 352
+SPARE = 16
+PLAIN = (384, 768)
+W_LOADS = [(Y, 0, 128), (Y, 128, 256), (E, 0, 256), (H, 0, 256)]
 
 
 def entries(lst, lo, hi):
@@ -53,17 +54,14 @@ def tile_picked_edgeatt_tanh_e_kernel(tc, xT, w1, w2, w3, offs, src, dst, out):
                 nc.sync.dma_start(offs_t[:], offs)
         w_raw = {}
         for i, lo, hi in W_LOADS:
-            if (i, lo) == (E, 0):
-                raw = reuse.tile([P, PACK, hi - lo], F32, name="we0_raw", offset=20480, align_bytes=64)
-            else:
-                raw = keep.tile([P, PACK, hi - lo], F32, name="w_raw%d_%d" % (i, lo))
+            raw = keep.tile([P, PACK, hi - lo], F32, name="w_raw%d_%d" % (i, lo))
             nc.sync.dma_start(out=raw[:], in_=(w1, w2, w3)[i].rearrange("(p j) n -> p j n", j=PACK)[:, :, lo:hi])
             for b in range(lo // P, hi // P):
                 w_raw[i, b] = (raw, b * P - lo)
         nc.sync.dma_start(dst_t[:], dst)
         nc.sync.dma_start(src_t[:], src)
 
-        x_bf = keep.tile([P, PACK * S], BF16, name="x_bf", align_bytes=64)
+        x_bf = chain.tile([P, PACK * S], BF16, name="x_bf", offset=0, align_bytes=64)
         x_slots = x_bf[:].rearrange("p (n j) -> p n j", j=PACK)
         x_codes = keep.tile([P, S], U32, name="x_codes", align_bytes=64)
         x_scales = keep.tile([P, S], U8, name="x_scales", align_bytes=64)
@@ -72,11 +70,14 @@ def tile_picked_edgeatt_tanh_e_kernel(tc, xT, w1, w2, w3, offs, src, dst, out):
         late_planes = late[:].rearrange("p (e n) -> p e n", e=2)
 
         res = {}
-        res[E, 0] = reuse.tile([P, S + E_SPARE], F32, name="e0", offset=0, align_bytes=64)
-        res[Y, 1] = reuse.tile([P, S], F32, name="y1", offset=8192, align_bytes=64)
-        zeros = keep.tile([P, E_SPARE], F32, name="zeros")
+        res[Y, 0] = keep.tile([P, S + COPY_SPARE], F32, name="y0")
+        res[E, 0] = reuse.tile([P, S + SPARE], F32, name="e0", offset=0, align_bytes=64)
+        res[Y, 1] = reuse.tile([P, S + SPARE], F32, name="y1", offset=8192, align_bytes=64)
+        res[E, 1] = keep.tile([P, S + SPARE], F32, name="e1")
+        zeros = keep.tile([P, COPY_SPARE], F32, name="zeros")
         nc.gpsimd.memset(zeros[:], 0.0)
-        nc.scalar.activation(res[E, 0][:, S:], zeros[:], TANH)
+        for window in res.values():
+            nc.scalar.activation(window[:, S:], zeros[:, : window.shape[1] - S], TANH)
 
         def pick_v(dest, j, lo, hi):
             nc.vector.tensor_copy(out=dest, in_=rows[j][:].indirect(entries(offs_t, lo, hi)))
@@ -84,11 +85,11 @@ def tile_picked_edgeatt_tanh_e_kernel(tc, xT, w1, w2, w3, offs, src, dst, out):
         def pick_s(dest, j, lo, hi):
             nc.scalar.activation(dest, rows[j][:].indirect(entries(offs_t, lo, hi)), COPY)
 
-        def insert(planes, first, lo, hi):
-            nc.vector.tensor_copy(out=x_slots[:, lo:hi, first : first + 2], in_=planes.rearrange("p e n -> p n e"))
+        def insert(planes, first, lo, hi, copy=nc.vector.tensor_copy):
+            copy(x_slots[:, lo:hi, first : first + 2], planes.rearrange("p e n -> p n e"))
 
-        def insert_late(lo, hi):
-            insert(late_planes[:, :, lo - DIRECT : hi - DIRECT], 2, lo, hi)
+        def insert_late(lo, hi, copy=nc.vector.tensor_copy):
+            insert(late_planes[:, :, lo - DIRECT : hi - DIRECT], 2, lo, hi, copy)
 
         def quantise_x(lo, hi):
             nc.vector.quantize_mx(
@@ -104,9 +105,10 @@ def tile_picked_edgeatt_tanh_e_kernel(tc, xT, w1, w2, w3, offs, src, dst, out):
             return grouped, raw[:, :, first : first + P].rearrange("p j (c n) -> p c j n", n=4)
 
         def interleave_gpsimd(dest, i, b):
+            raw, first = w_raw[i, b]
             nc.gpsimd.tensor_scalar(
                 dest[:].rearrange("p (n j) -> p n j", j=PACK),
-                w_raw[i, b][0][:].rearrange("p j n -> p n j"),
+                raw[:, :, first : first + P].rearrange("p j n -> p n j"),
                 1.0,
                 0.0,
                 MULT,
@@ -123,7 +125,7 @@ def tile_picked_edgeatt_tanh_e_kernel(tc, xT, w1, w2, w3, offs, src, dst, out):
                 w_codes[block] = codes[:, P * place : P * (place + 1)]
                 w_scales[block] = scales[:, P * place : P * (place + 1)]
 
-        def product(i, b, first, last, bank, width=512):
+        def product(i, b, first, last, bank, width=512, copy=nc.scalar.copy):
             acc = psum.tile([P, last - first], F32, name="acc", tag="bank%d" % bank)
             for lo in range(first, last, width):
                 hi = min(lo + width, last)
@@ -136,7 +138,7 @@ def tile_picked_edgeatt_tanh_e_kernel(tc, xT, w1, w2, w3, offs, src, dst, out):
                     start=True,
                     stop=True,
                 )
-            nc.scalar.copy(res[i, b][:, first:last], acc[:])
+            copy(res[i, b][:, first:last], acc[:])
 
         def send(b, gate, lo, hi):
             message = keep.tile([P, hi - lo], F32, name="message%d_%d" % (b, lo))
@@ -153,81 +155,65 @@ def tile_picked_edgeatt_tanh_e_kernel(tc, xT, w1, w2, w3, offs, src, dst, out):
         pick_v(x_slots[:, :DIRECT, 3], 3, 0, DIRECT)
         for lo, hi in STEPS[1:]:
             pick_s(late_planes[:, 1, lo - DIRECT : hi - DIRECT], 3, lo, hi)
-        first_bf = keep.tile([P, PACK * P], BF16, name="first_bf", align_bytes=64)
-        second_bf = chain.tile([P, 2 * PACK * P], BF16, name="second_bf", offset=2560, align_bytes=64)
-        nc.scalar.copy(*grouped_views(second_bf[:, : PACK * P], Y, 1))
-        nc.scalar.copy(*grouped_views(second_bf[:, PACK * P :], E, 0))
+        wy_bf = [keep.tile([P, PACK * P], BF16, name="wy_bf%d" % b, align_bytes=64) for b in range(2)]
+        insert_late(*STEPS[2], nc.scalar.copy)
+        nc.scalar.copy(*grouped_views(wy_bf[1][:], Y, 1))
 
+        nc.vector.tensor_copy(*grouped_views(wy_bf[0][:], Y, 0))
         insert_late(*STEPS[1])
-        nc.vector.tensor_copy(*grouped_views(first_bf[:], Y, 0))
+        quantise_w(wy_bf[0], [(Y, 0)])
         quantise_x(*STEPS[0])
-        quantise_w(first_bf, [(Y, 0)])
-        insert_late(*STEPS[2])
-        quantise_x(*STEPS[1])
         insert_late(*STEPS[3])
-        quantise_x(*STEPS[2])
+        quantise_x(*STEPS[1])
         quantise_x(*STEPS[3])
-        quantise_w(second_bf, [(Y, 1), (E, 0)])
-        we1_bf = chain.tile([P, PACK * P], BF16, name="we1_bf", offset=2560, align_bytes=64)
+        quantise_x(*STEPS[2])
+        quantise_w(wy_bf[1], [(Y, 1)])
+        we0_bf = chain.tile([P, PACK * P], BF16, name="we0_bf", offset=2048, align_bytes=64)
+        we1_bf = chain.tile([P, PACK * P], BF16, name="we1_bf", offset=3072, align_bytes=64)
+        nc.vector.tensor_copy(*grouped_views(we0_bf[:], E, 0))
         nc.vector.tensor_copy(*grouped_views(we1_bf[:], E, 1))
+        quantise_w(we0_bf, [(E, 0)])
         quantise_w(we1_bf, [(E, 1)])
 
-        res[Y, 0] = reuse.tile([P, S], F32, name="y0", offset=20480, align_bytes=64)
         product(Y, 0, *HALVES[0], 0, 256)
-        product(Y, 0, *STEPS[2], 1)
-        product(Y, 0, *STEPS[3], 2)
-        at_dst0 = keep.tile([P, U], F32, name="at_dst0")
-        for lo, hi in HALVES:
-            nc.vector.tensor_copy(out=at_dst0[:, lo:hi], in_=res[Y, 0][:].indirect(entries(dst_t, lo, hi)))
+        product(Y, 0, *STEPS[3], 1)
+        product(Y, 0, *STEPS[2], 2)
+        at_dst = [keep.tile([P, U], F32, name="at_dst%d" % b) for b in range(2)]
+        nc.vector.tensor_copy(out=at_dst[0][:], in_=res[Y, 0][:].indirect(dst_t[:]))
 
-        wh_bf = chain.tile([P, PACK * N], BF16, name="wh_bf", offset=3328, align_bytes=64)
-        interleave_gpsimd(wh_bf, H, 0)
-        quantise_w(wh_bf, [(H, 0), (H, 1)])
+        wh0_bf = chain.tile([P, PACK * P], BF16, name="wh0_bf", offset=3584, align_bytes=64)
+        wh1_bf = chain.tile([P, PACK * P], BF16, name="wh1_bf", offset=2560, align_bytes=64)
+        interleave_gpsimd(wh0_bf, H, 0)
+        interleave_gpsimd(wh1_bf, H, 1)
+        quantise_w(wh0_bf, [(H, 0)])
+        quantise_w(wh1_bf, [(H, 1)])
 
         product(Y, 1, *HALVES[0], 3)
         product(Y, 1, *HALVES[1], 4)
         product(E, 0, *HALVES[0], 5)
         product(E, 0, *HALVES[1], 6)
-        summed0 = chain.tile([P, U], F32, name="summed0", offset=5120, align_bytes=64)
-        nc.vector.tensor_tensor(summed0[:], res[E, 0][:].indirect(src_t[:]), at_dst0[:], ADD)
-
-        res[E, 1] = keep.tile([P, S], F32, name="e1")
-        summed1 = chain.tile([P, U], F32, name="summed1", offset=0, align_bytes=64)
-        at_dst1 = [
-            keep.tile([P, 512], F32, name="at_dst1a"),
-            keep.tile([P, 512], F32, name="at_dst1b"),
-        ]
-
-        def fetch_dst1(half):
-            nc.scalar.activation(at_dst1[half][:], res[Y, 1][:].indirect(entries(dst_t, *HALVES[half])), COPY)
-
-        def add_src1(half):
-            lo, hi = HALVES[half]
-            nc.vector.tensor_tensor(
-                summed1[:, lo:hi], res[E, 1][:].indirect(entries(src_t, lo, hi)), at_dst1[half][:], ADD
-            )
-
         product(E, 1, *HALVES[0], 7)
-        product(E, 1, *HALVES[1], 0)
-        fetch_dst1(0)
-        fetch_dst1(1)
-        add_src1(0)
-        add_src1(1)
+        product(E, 1, *STEPS[2], 0)
+        product(E, 1, *STEPS[3], 1, copy=nc.vector.tensor_copy)
+        nc.scalar.activation(at_dst[1][:], res[Y, 1][:].indirect(dst_t[:]), COPY)
+        summed0 = chain.tile([P, U], F32, name="summed0", offset=4096, align_bytes=64)
+        summed1 = keep.tile([P, U], F32, name="summed1")
+        nc.vector.tensor_tensor(summed0[:], res[E, 0][:].indirect(src_t[:]), at_dst[0][:], ADD)
+        nc.vector.tensor_tensor(summed1[:], res[E, 1][:].indirect(src_t[:]), at_dst[1][:], ADD)
 
         res[H, 0] = keep.tile([P, S], F32, name="h0")
-        product(H, 0, *HALVES[0], 7)
-        product(H, 0, *HALVES[1], 0)
+        product(H, 0, *HALVES[0], 0)
+        product(H, 0, *HALVES[1], 7)
         gate0 = reuse.tile([P, U], F32, name="gate0", offset=8192, align_bytes=64)
         for lo, hi in HALVES:
             nc.scalar.activation(gate0[:, lo:hi], summed0[:, lo:hi], TANH)
             send(0, gate0, lo, hi)
 
         res[H, 1] = reuse.tile([P, S], F32, name="h1", offset=0, align_bytes=64)
-        product(H, 1, *HALVES[0], 1)
+        product(H, 1, *HALVES[0], 3)
         product(H, 1, *HALVES[1], 2)
         gate1 = keep.tile([P, U], F32, name="gate1")
-        for lo, hi in HALVES:
-            nc.scalar.activation(gate1[:, lo:hi], summed1[:, lo:hi], TANH)
+        nc.scalar.activation(gate1[:], summed1[:], TANH)
         lo, hi = PLAIN
         send(1, gate1, 0, lo)
         at_src = keep.tile([P, hi - lo], F32, name="at_src")

@@ -188,13 +188,14 @@ def tile_picked_edgeatt_tanh_e_kernel(tc, xT, w1, w2, w3, offs, src, dst, out):
         quantise_w(wh0_bf, [(H, 0)])
         quantise_w(wh1_bf, [(H, 1)])
 
-        product(Y, 1, *HALVES[0], 3)
-        product(Y, 1, *HALVES[1], 4)
-        product(E, 0, *HALVES[0], 5)
-        product(E, 0, *HALVES[1], 6)
-        product(E, 1, *HALVES[0], 7)
-        product(E, 1, *STEPS[2], 0)
-        product(E, 1, *STEPS[3], 1, copy=nc.vector.tensor_copy)
+        product(Y, 1, 0, 256, 3)
+        product(Y, 1, 256, 768, 4)
+        product(Y, 1, 768, S, 5)
+        product(E, 0, *HALVES[0], 6)
+        product(E, 0, *HALVES[1], 7)
+        product(E, 1, *HALVES[0], 0)
+        product(E, 1, *STEPS[2], 1)
+        product(E, 1, *STEPS[3], 2, copy=nc.vector.tensor_copy)
         nc.scalar.activation(at_dst[1][:], res[Y, 1][:].indirect(dst_t[:]), COPY)
         summed0 = chain.tile([P, U], F32, name="summed0", offset=4096, align_bytes=64)
         summed1 = keep.tile([P, U], F32, name="summed1")
@@ -202,8 +203,8 @@ def tile_picked_edgeatt_tanh_e_kernel(tc, xT, w1, w2, w3, offs, src, dst, out):
         nc.vector.tensor_tensor(summed1[:], res[E, 1][:].indirect(src_t[:]), at_dst[1][:], ADD)
 
         res[H, 0] = keep.tile([P, S], F32, name="h0")
-        product(H, 0, *HALVES[0], 0)
-        product(H, 0, *HALVES[1], 7)
+        product(H, 0, *HALVES[0], 1)
+        product(H, 0, *HALVES[1], 0)
         gate0 = reuse.tile([P, U], F32, name="gate0", offset=8192, align_bytes=64)
         for lo, hi in HALVES:
             nc.scalar.activation(gate0[:, lo:hi], summed0[:, lo:hi], TANH)
@@ -211,10 +212,11 @@ def tile_picked_edgeatt_tanh_e_kernel(tc, xT, w1, w2, w3, offs, src, dst, out):
 
         res[H, 1] = reuse.tile([P, S], F32, name="h1", offset=0, align_bytes=64)
         product(H, 1, *HALVES[0], 3)
-        product(H, 1, *HALVES[1], 2)
+        product(H, 1, *HALVES[1], 4)
         gate1 = keep.tile([P, U], F32, name="gate1")
-        nc.scalar.activation(gate1[:], summed1[:], TANH)
         lo, hi = PLAIN
+        nc.scalar.activation(gate1[:, :lo], summed1[:, :lo], TANH)
+        nc.scalar.activation(gate1[:, lo:], summed1[:, lo:], TANH)
         send(1, gate1, 0, lo)
         at_src = keep.tile([P, hi - lo], F32, name="at_src")
         nc.scalar.activation(at_src[:], res[H, 1][:].indirect(entries(src_t, lo, hi)), COPY)

@@ -19,7 +19,7 @@ COPY = mybir.ActivationFunctionType.Copy
 P = 128
 PACK = 4
 LIST_ROWS = 16
-Y, E, H = 0, 1, 2
+E, Y, H = 0, 1, 2
 
 DIRECT = 256
 STEPS = [(0, 256), (256, 512), (512, 768), (768, 1024)]
@@ -27,7 +27,7 @@ HALVES = [(0, 512), (512, 1024)]
 COPY_SPARE = 352
 SPARE = 16
 PLAIN = (384, 768)
-W_LOADS = [(Y, 0, 128), (Y, 128, 256), (E, 0, 256), (H, 0, 256)]
+W_LOADS = [(E, 0, 128), (E, 128, 256), (Y, 0, 256), (H, 0, 256)]
 
 
 def entries(lst, lo, hi):
@@ -55,11 +55,11 @@ def tile_picked_edgeatt_tanh_e_kernel(tc, xT, w1, w2, w3, offs, src, dst, out):
         w_raw = {}
         for i, lo, hi in W_LOADS:
             raw = keep.tile([P, PACK, hi - lo], F32, name="w_raw%d_%d" % (i, lo))
-            nc.sync.dma_start(out=raw[:], in_=(w1, w2, w3)[i].rearrange("(p j) n -> p j n", j=PACK)[:, :, lo:hi])
+            nc.sync.dma_start(out=raw[:], in_=(w2, w1, w3)[i].rearrange("(p j) n -> p j n", j=PACK)[:, :, lo:hi])
             for b in range(lo // P, hi // P):
                 w_raw[i, b] = (raw, b * P - lo)
-        nc.sync.dma_start(dst_t[:], dst)
         nc.sync.dma_start(src_t[:], src)
+        nc.sync.dma_start(dst_t[:], dst)
 
         x_bf = chain.tile([P, PACK * S], BF16, name="x_bf", offset=0, align_bytes=64)
         x_slots = x_bf[:].rearrange("p (n j) -> p n j", j=PACK)
@@ -70,10 +70,10 @@ def tile_picked_edgeatt_tanh_e_kernel(tc, xT, w1, w2, w3, offs, src, dst, out):
         late_planes = late[:].rearrange("p (e n) -> p e n", e=2)
 
         res = {}
-        res[Y, 0] = keep.tile([P, S + COPY_SPARE], F32, name="y0")
-        res[E, 0] = reuse.tile([P, S + SPARE], F32, name="e0", offset=0, align_bytes=64)
-        res[Y, 1] = reuse.tile([P, S + SPARE], F32, name="y1", offset=8192, align_bytes=64)
-        res[E, 1] = keep.tile([P, S + SPARE], F32, name="e1")
+        res[E, 0] = keep.tile([P, S + COPY_SPARE], F32, name="e0")
+        res[Y, 0] = reuse.tile([P, S + SPARE], F32, name="y0", offset=0, align_bytes=64)
+        res[E, 1] = reuse.tile([P, S + SPARE], F32, name="e1", offset=8192, align_bytes=64)
+        res[Y, 1] = keep.tile([P, S + SPARE], F32, name="y1")
         zeros = keep.tile([P, COPY_SPARE], F32, name="zeros")
         nc.gpsimd.memset(zeros[:], 0.0)
         for window in res.values():
@@ -155,31 +155,30 @@ def tile_picked_edgeatt_tanh_e_kernel(tc, xT, w1, w2, w3, offs, src, dst, out):
         pick_v(x_slots[:, :DIRECT, 3], 3, 0, DIRECT)
         for lo, hi in STEPS[1:]:
             pick_s(late_planes[:, 1, lo - DIRECT : hi - DIRECT], 3, lo, hi)
-        wy_bf = [keep.tile([P, PACK * P], BF16, name="wy_bf%d" % b, align_bytes=64) for b in range(2)]
+        we_bf = [keep.tile([P, PACK * P], BF16, name="we_bf%d" % b, align_bytes=64) for b in range(2)]
         insert_late(*STEPS[2], nc.scalar.copy)
-        nc.scalar.copy(*grouped_views(wy_bf[1][:], Y, 1))
+        nc.scalar.copy(*grouped_views(we_bf[1][:], E, 1))
 
-        nc.vector.tensor_copy(*grouped_views(wy_bf[0][:], Y, 0))
+        nc.vector.tensor_copy(*grouped_views(we_bf[0][:], E, 0))
         insert_late(*STEPS[1])
-        quantise_w(wy_bf[0], [(Y, 0)])
+        quantise_w(we_bf[0], [(E, 0)])
         quantise_x(*STEPS[0])
         insert_late(*STEPS[3])
         quantise_x(*STEPS[1])
         quantise_x(*STEPS[3])
         quantise_x(*STEPS[2])
-        quantise_w(wy_bf[1], [(Y, 1)])
-        we0_bf = chain.tile([P, PACK * P], BF16, name="we0_bf", offset=2048, align_bytes=64)
-        we1_bf = chain.tile([P, PACK * P], BF16, name="we1_bf", offset=3072, align_bytes=64)
-        nc.vector.tensor_copy(*grouped_views(we0_bf[:], E, 0))
-        nc.vector.tensor_copy(*grouped_views(we1_bf[:], E, 1))
-        quantise_w(we0_bf, [(E, 0)])
-        quantise_w(we1_bf, [(E, 1)])
+        quantise_w(we_bf[1], [(E, 1)])
+        wy0_bf = chain.tile([P, PACK * P], BF16, name="wy0_bf", offset=2048, align_bytes=64)
+        wy1_bf = chain.tile([P, PACK * P], BF16, name="wy1_bf", offset=3072, align_bytes=64)
+        nc.vector.tensor_copy(*grouped_views(wy0_bf[:], Y, 0))
+        nc.vector.tensor_copy(*grouped_views(wy1_bf[:], Y, 1))
+        quantise_w(wy0_bf, [(Y, 0)])
+        quantise_w(wy1_bf, [(Y, 1)])
 
-        product(Y, 0, *HALVES[0], 0, 256)
-        product(Y, 0, *STEPS[3], 1)
-        product(Y, 0, *STEPS[2], 2)
-        at_dst = [keep.tile([P, U], F32, name="at_dst%d" % b) for b in range(2)]
-        nc.vector.tensor_copy(out=at_dst[0][:], in_=res[Y, 0][:].indirect(dst_t[:]))
+        for bank, step in enumerate((0, 1, 3, 2)):
+            product(E, 0, *STEPS[step], bank)
+        fetched = [keep.tile([P, U], F32, name="fetched%d" % b) for b in range(2)]
+        nc.vector.tensor_copy(out=fetched[0][:], in_=res[E, 0][:].indirect(src_t[:]))
 
         wh0_bf = chain.tile([P, PACK * P], BF16, name="wh0_bf", offset=3584, align_bytes=64)
         wh1_bf = chain.tile([P, PACK * P], BF16, name="wh1_bf", offset=2560, align_bytes=64)
@@ -188,31 +187,30 @@ def tile_picked_edgeatt_tanh_e_kernel(tc, xT, w1, w2, w3, offs, src, dst, out):
         quantise_w(wh0_bf, [(H, 0)])
         quantise_w(wh1_bf, [(H, 1)])
 
-        product(Y, 1, 0, 256, 3)
-        product(Y, 1, 256, 768, 4)
-        product(Y, 1, 768, S, 5)
-        product(E, 0, *HALVES[0], 6)
-        product(E, 0, *HALVES[1], 7)
-        product(E, 1, *HALVES[0], 0)
-        product(E, 1, *STEPS[2], 1)
-        product(E, 1, *STEPS[3], 2, copy=nc.vector.tensor_copy)
-        nc.scalar.activation(at_dst[1][:], res[Y, 1][:].indirect(dst_t[:]), COPY)
+        for step, (lo, hi) in enumerate(STEPS):
+            product(E, 1, lo, hi, 4 + step)
+        product(Y, 0, *HALVES[0], 0)
+        product(Y, 0, *HALVES[1], 1)
+        product(Y, 1, *HALVES[0], 2)
+        product(Y, 1, *STEPS[2], 3)
+        product(Y, 1, *STEPS[3], 4, copy=nc.vector.tensor_copy)
+        nc.scalar.activation(fetched[1][:], res[E, 1][:].indirect(src_t[:]), COPY)
         summed0 = chain.tile([P, U], F32, name="summed0", offset=4096, align_bytes=64)
         summed1 = keep.tile([P, U], F32, name="summed1")
-        nc.vector.tensor_tensor(summed0[:], res[E, 0][:].indirect(src_t[:]), at_dst[0][:], ADD)
-        nc.vector.tensor_tensor(summed1[:], res[E, 1][:].indirect(src_t[:]), at_dst[1][:], ADD)
+        nc.vector.tensor_tensor(summed0[:], res[Y, 0][:].indirect(dst_t[:]), fetched[0][:], ADD)
+        nc.vector.tensor_tensor(summed1[:], res[Y, 1][:].indirect(dst_t[:]), fetched[1][:], ADD)
 
         res[H, 0] = keep.tile([P, S], F32, name="h0")
-        product(H, 0, *HALVES[0], 1)
-        product(H, 0, *HALVES[1], 0)
+        product(H, 0, *HALVES[0], 3)
+        product(H, 0, *HALVES[1], 2)
         gate0 = reuse.tile([P, U], F32, name="gate0", offset=8192, align_bytes=64)
         for lo, hi in HALVES:
             nc.scalar.activation(gate0[:, lo:hi], summed0[:, lo:hi], TANH)
             send(0, gate0, lo, hi)
 
         res[H, 1] = reuse.tile([P, S], F32, name="h1", offset=0, align_bytes=64)
-        product(H, 1, *HALVES[0], 3)
-        product(H, 1, *HALVES[1], 4)
+        product(H, 1, *HALVES[0], 5)
+        product(H, 1, *HALVES[1], 6)
         gate1 = keep.tile([P, U], F32, name="gate1")
         lo, hi = PLAIN
         nc.scalar.activation(gate1[:, :lo], summed1[:, :lo], TANH)

@@ -24,6 +24,7 @@ E, Y, H = 0, 1, 2
 DIRECT = 256
 STEPS = [(0, 256), (256, 512), (512, 768), (768, 1024)]
 HALVES = [(0, 512), (512, 1024)]
+LATE_PICKS = [(256, 768), (768, 1024)]
 COPY_SPARE = 352
 SPARE = 16
 PLAIN = (384, 768)
@@ -54,7 +55,10 @@ def tile_picked_edgeatt_tanh_e_kernel(tc, xT, w1, w2, w3, offs, src, dst, out):
                 nc.sync.dma_start(offs_t[:], offs)
         w_raw = {}
         for i, lo, hi in W_LOADS:
-            raw = keep.tile([P, PACK, hi - lo], F32, name="w_raw%d_%d" % (i, lo))
+            if i == H:
+                raw = reuse.tile([P, PACK, hi - lo], F32, name="wh_raw", offset=16384, align_bytes=64)
+            else:
+                raw = keep.tile([P, PACK, hi - lo], F32, name="w_raw%d_%d" % (i, lo))
             nc.sync.dma_start(out=raw[:], in_=(w2, w1, w3)[i].rearrange("(p j) n -> p j n", j=PACK)[:, :, lo:hi])
             for b in range(lo // P, hi // P):
                 w_raw[i, b] = (raw, b * P - lo)
@@ -108,7 +112,7 @@ def tile_picked_edgeatt_tanh_e_kernel(tc, xT, w1, w2, w3, offs, src, dst, out):
             raw, first = w_raw[i, b]
             nc.gpsimd.tensor_scalar(
                 dest[:].rearrange("p (n j) -> p n j", j=PACK),
-                raw[:, :, first : first + P].rearrange("p j n -> p n j"),
+                raw[:, :, first : first + dest.shape[1] // PACK].rearrange("p j n -> p n j"),
                 1.0,
                 0.0,
                 MULT,
@@ -153,16 +157,16 @@ def tile_picked_edgeatt_tanh_e_kernel(tc, xT, w1, w2, w3, offs, src, dst, out):
         pick_s(late_planes[:, 0, :], 2, DIRECT, S)
 
         pick_v(x_slots[:, :DIRECT, 3], 3, 0, DIRECT)
-        for lo, hi in STEPS[1:]:
+        for lo, hi in LATE_PICKS:
             pick_s(late_planes[:, 1, lo - DIRECT : hi - DIRECT], 3, lo, hi)
         we_bf = [keep.tile([P, PACK * P], BF16, name="we_bf%d" % b, align_bytes=64) for b in range(2)]
         insert_late(*STEPS[2], nc.scalar.copy)
         nc.scalar.copy(*grouped_views(we_bf[1][:], E, 1))
 
         nc.vector.tensor_copy(*grouped_views(we_bf[0][:], E, 0))
+        quantise_x(*STEPS[0])
         insert_late(*STEPS[1])
         quantise_w(we_bf[0], [(E, 0)])
-        quantise_x(*STEPS[0])
         insert_late(*STEPS[3])
         quantise_x(*STEPS[1])
         quantise_x(*STEPS[3])
@@ -180,12 +184,9 @@ def tile_picked_edgeatt_tanh_e_kernel(tc, xT, w1, w2, w3, offs, src, dst, out):
         fetched = [keep.tile([P, U], F32, name="fetched%d" % b) for b in range(2)]
         nc.vector.tensor_copy(out=fetched[0][:], in_=res[E, 0][:].indirect(src_t[:]))
 
-        wh0_bf = chain.tile([P, PACK * P], BF16, name="wh0_bf", offset=3584, align_bytes=64)
-        wh1_bf = chain.tile([P, PACK * P], BF16, name="wh1_bf", offset=2560, align_bytes=64)
-        interleave_gpsimd(wh0_bf, H, 0)
-        interleave_gpsimd(wh1_bf, H, 1)
-        quantise_w(wh0_bf, [(H, 0)])
-        quantise_w(wh1_bf, [(H, 1)])
+        wh_bf = chain.tile([P, PACK * N], BF16, name="wh_bf", offset=3584, align_bytes=64)
+        interleave_gpsimd(wh_bf, H, 0)
+        quantise_w(wh_bf, [(H, 0), (H, 1)])
 
         for step, (lo, hi) in enumerate(STEPS):
             product(E, 1, lo, hi, 4 + step)
@@ -195,7 +196,7 @@ def tile_picked_edgeatt_tanh_e_kernel(tc, xT, w1, w2, w3, offs, src, dst, out):
         product(Y, 1, *STEPS[2], 3)
         product(Y, 1, *STEPS[3], 4, copy=nc.vector.tensor_copy)
         nc.scalar.activation(fetched[1][:], res[E, 1][:].indirect(src_t[:]), COPY)
-        summed0 = chain.tile([P, U], F32, name="summed0", offset=4096, align_bytes=64)
+        summed0 = reuse.tile([P, U], F32, name="summed0", offset=16384, align_bytes=64)
         summed1 = keep.tile([P, U], F32, name="summed1")
         nc.vector.tensor_tensor(summed0[:], res[Y, 0][:].indirect(dst_t[:]), fetched[0][:], ADD)
         nc.vector.tensor_tensor(summed1[:], res[Y, 1][:].indirect(dst_t[:]), fetched[1][:], ADD)

@@ -28,6 +28,7 @@ LATE_PICKS = [(256, 768), (768, 1024)]
 COPY_SPARE = 352
 SPARE = 16
 PLAIN = (384, 768)
+VECTOR_COLUMNS = 64
 W_LOADS = [(E, 0, 128), (E, 128, 256), (Y, 0, 256), (H, 0, 256)]
 
 
@@ -39,7 +40,6 @@ def tile_picked_edgeatt_tanh_e_kernel(tc, xT, w1, w2, w3, offs, src, dst, out):
     nc = tc.nc
     with ExitStack() as ctx:
         keep = ctx.enter_context(tc.tile_pool(name="keep", bufs=1))
-        chain = ctx.enter_context(tc.tile_pool(name="chain", bufs=1))
         reuse = ctx.enter_context(tc.tile_pool(name="reuse", bufs=1))
         psum = ctx.enter_context(tc.psum_pool(name="psum", bufs=1))
 
@@ -65,7 +65,7 @@ def tile_picked_edgeatt_tanh_e_kernel(tc, xT, w1, w2, w3, offs, src, dst, out):
         nc.sync.dma_start(src_t[:], src)
         nc.sync.dma_start(dst_t[:], dst)
 
-        x_bf = chain.tile([P, PACK * S], BF16, name="x_bf", offset=0, align_bytes=64)
+        x_bf = keep.tile([P, PACK * S], BF16, name="x_bf", align_bytes=64)
         x_slots = x_bf[:].rearrange("p (n j) -> p n j", j=PACK)
         x_codes = keep.tile([P, S], U32, name="x_codes", align_bytes=64)
         x_scales = keep.tile([P, S], U8, name="x_scales", align_bytes=64)
@@ -106,25 +106,14 @@ def tile_picked_edgeatt_tanh_e_kernel(tc, xT, w1, w2, w3, offs, src, dst, out):
         def grouped_views(dest, i, b):
             grouped = dest.rearrange("p (c n j) -> p c j n", n=4, j=PACK)
             raw, first = w_raw[i, b]
-            return grouped, raw[:, :, first : first + P].rearrange("p j (c n) -> p c j n", n=4)
-
-        def interleave_gpsimd(dest, i, b):
-            raw, first = w_raw[i, b]
-            nc.gpsimd.tensor_scalar(
-                dest[:].rearrange("p (n j) -> p n j", j=PACK),
-                raw[:, :, first : first + dest.shape[1] // PACK].rearrange("p j n -> p n j"),
-                1.0,
-                0.0,
-                MULT,
-                ADD,
-            )
+            return grouped, raw[:, :, first : first + dest.shape[1] // PACK].rearrange("p j (c n) -> p c j n", n=4)
 
         def quantise_w(source, blocks, codes=None):
             width = P * len(blocks)
             if codes is None:
                 codes = keep.tile([P, width], U32, name="w_codes%d_%d" % blocks[0], align_bytes=64)
             scales = keep.tile([P, width], U8, name="w_scales%d_%d" % blocks[0], align_bytes=64)
-            nc.vector.quantize_mx(out=codes[:].bitcast(FP8X4), scales=scales[:], in_=source[:])
+            nc.vector.quantize_mx(out=codes[:].bitcast(FP8X4), scales=scales[:], in_=source)
             for place, block in enumerate(blocks):
                 w_codes[block] = codes[:, P * place : P * (place + 1)]
                 w_scales[block] = scales[:, P * place : P * (place + 1)]
@@ -166,17 +155,19 @@ def tile_picked_edgeatt_tanh_e_kernel(tc, xT, w1, w2, w3, offs, src, dst, out):
         nc.vector.tensor_copy(*grouped_views(we_bf[0][:], E, 0))
         quantise_x(*STEPS[0])
         insert_late(*STEPS[1])
-        quantise_w(we_bf[0], [(E, 0)])
+        quantise_w(we_bf[0][:], [(E, 0)])
         insert_late(*STEPS[3])
         quantise_x(*STEPS[1])
         quantise_x(*STEPS[3])
         quantise_x(*STEPS[2])
-        quantise_w(we_bf[1], [(E, 1)])
-        wy0_bf = chain.tile([P, PACK * P], BF16, name="wy0_bf", offset=2048, align_bytes=64)
-        wy1_bf = chain.tile([P, PACK * P], BF16, name="wy1_bf", offset=3072, align_bytes=64)
+        quantise_w(we_bf[1][:], [(E, 1)])
+        wy0_bf = keep.tile([P, PACK * P], BF16, name="wy0_bf", align_bytes=64)
+        wh_bf = keep.tile([P, PACK * N], BF16, name="wh_bf", align_bytes=64)
+        wy1_bf = wh_bf[:, PACK * P :]
         nc.vector.tensor_copy(*grouped_views(wy0_bf[:], Y, 0))
-        nc.vector.tensor_copy(*grouped_views(wy1_bf[:], Y, 1))
-        quantise_w(wy0_bf, [(Y, 0)])
+        nc.vector.tensor_copy(*grouped_views(wy1_bf, Y, 1))
+        nc.vector.tensor_copy(*grouped_views(wh_bf[:, : PACK * VECTOR_COLUMNS], H, 0))
+        quantise_w(wy0_bf[:], [(Y, 0)])
         quantise_w(wy1_bf, [(Y, 1)])
 
         for bank, step in enumerate((0, 1, 3, 2)):
@@ -184,17 +175,24 @@ def tile_picked_edgeatt_tanh_e_kernel(tc, xT, w1, w2, w3, offs, src, dst, out):
         fetched = [keep.tile([P, U], F32, name="fetched%d" % b) for b in range(2)]
         nc.vector.tensor_copy(out=fetched[0][:], in_=res[E, 0][:].indirect(src_t[:]))
 
-        wh_bf = chain.tile([P, PACK * N], BF16, name="wh_bf", offset=3584, align_bytes=64)
-        interleave_gpsimd(wh_bf, H, 0)
-        quantise_w(wh_bf, [(H, 0), (H, 1)])
+        nc.gpsimd.tensor_scalar(
+            wh_bf[:, PACK * VECTOR_COLUMNS :].rearrange("p (n j) -> p n j", j=PACK),
+            w_raw[H, 0][0][:, :, VECTOR_COLUMNS:].rearrange("p j n -> p n j"),
+            1.0,
+            0.0,
+            MULT,
+            ADD,
+        )
+        quantise_w(wh_bf[:], [(H, 0), (H, 1)])
 
         for step, (lo, hi) in enumerate(STEPS):
             product(E, 1, lo, hi, 4 + step)
-        product(Y, 0, *HALVES[0], 0)
-        product(Y, 0, *HALVES[1], 1)
-        product(Y, 1, *HALVES[0], 2)
-        product(Y, 1, *STEPS[2], 3)
-        product(Y, 1, *STEPS[3], 4, copy=nc.vector.tensor_copy)
+        product(Y, 0, *STEPS[0], 0)
+        product(Y, 0, *STEPS[1], 1)
+        product(Y, 0, *HALVES[1], 2)
+        product(Y, 1, *HALVES[0], 3)
+        product(Y, 1, *STEPS[2], 4)
+        product(Y, 1, *STEPS[3], 5, copy=nc.vector.tensor_copy)
         nc.scalar.activation(fetched[1][:], res[E, 1][:].indirect(src_t[:]), COPY)
         summed0 = reuse.tile([P, U], F32, name="summed0", offset=16384, align_bytes=64)
         summed1 = keep.tile([P, U], F32, name="summed1")
@@ -202,15 +200,15 @@ def tile_picked_edgeatt_tanh_e_kernel(tc, xT, w1, w2, w3, offs, src, dst, out):
         nc.vector.tensor_tensor(summed1[:], res[Y, 1][:].indirect(dst_t[:]), fetched[1][:], ADD)
 
         res[H, 0] = keep.tile([P, S], F32, name="h0")
-        product(H, 0, *HALVES[0], 3)
-        product(H, 0, *HALVES[1], 2)
+        product(H, 0, *HALVES[0], 4)
+        product(H, 0, *HALVES[1], 3)
         gate0 = reuse.tile([P, U], F32, name="gate0", offset=8192, align_bytes=64)
         for lo, hi in HALVES:
             nc.scalar.activation(gate0[:, lo:hi], summed0[:, lo:hi], TANH)
             send(0, gate0, lo, hi)
 
         res[H, 1] = reuse.tile([P, S], F32, name="h1", offset=0, align_bytes=64)
-        product(H, 1, *HALVES[0], 5)
+        product(H, 1, *HALVES[0], 7)
         product(H, 1, *HALVES[1], 6)
         gate1 = keep.tile([P, U], F32, name="gate1")
         lo, hi = PLAIN

from contextlib import ExitStack

import concourse.mybir as mybir

K, T, S, N, U = 512, 2048, 1024, 256, 1024
FLOPS = 3 * 2 * K * N * S

F32 = mybir.dt.float32
BF16 = mybir.dt.bfloat16
U32 = mybir.dt.uint32
U16 = mybir.dt.uint16
U8 = mybir.dt.uint8
FP8X4 = mybir.dt.float8_e4m3fn_x4
ADD = mybir.AluOpType.add
MULT = mybir.AluOpType.mult
TANH = mybir.ActivationFunctionType.Tanh
COPY = mybir.ActivationFunctionType.Copy

P = 128
PACK = 4
LIST_ROWS = 16
E, Y, H = 0, 1, 2

DIRECT = 256
STEPS = [(0, 256), (256, 512), (512, 768), (768, 1024)]
HALVES = [(0, 512), (512, 1024)]
LATE_PICKS = [(256, 768), (768, 1024)]
COPY_SPARE = 352
SPARE = 16
PLAIN = (384, 768)
VECTOR_COLUMNS = 64
W_LOADS = [(E, 0, 128), (E, 128, 256), (Y, 0, 256), (H, 0, 256)]


def entries(lst, lo, hi):
    return lst[:, lo // LIST_ROWS : hi // LIST_ROWS]


def tile_picked_edgeatt_tanh_e_kernel(tc, xT, w1, w2, w3, offs, src, dst, out):
    nc = tc.nc
    with ExitStack() as ctx:
        keep = ctx.enter_context(tc.tile_pool(name="keep", bufs=1))
        reuse = ctx.enter_context(tc.tile_pool(name="reuse", bufs=1))
        psum = ctx.enter_context(tc.psum_pool(name="psum", bufs=1))

        offs_t = keep.tile([P, S // LIST_ROWS], U16, name="offs_t")
        src_t = keep.tile([P, U // LIST_ROWS], U16, name="src_t")
        dst_t = keep.tile([P, U // LIST_ROWS], U16, name="dst_t")

        x_rows = xT.rearrange("(p j) t -> p j t", j=PACK)
        rows = [keep.tile([P, T], F32, name="row%d" % j) for j in range(PACK)]
        for j in range(PACK):
            nc.sync.dma_start(out=rows[j][:], in_=x_rows[:, j, :])
            if j == 0:
                nc.sync.dma_start(offs_t[:], offs)
        w_raw = {}
        for i, lo, hi in W_LOADS:
            if i == H:
                raw = reuse.tile([P, PACK, hi - lo], F32, name="wh_raw", offset=16384, align_bytes=64)
            else:
                raw = keep.tile([P, PACK, hi - lo], F32, name="w_raw%d_%d" % (i, lo))
            nc.sync.dma_start(out=raw[:], in_=(w2, w1, w3)[i].rearrange("(p j) n -> p j n", j=PACK)[:, :, lo:hi])
            for b in range(lo // P, hi // P):
                w_raw[i, b] = (raw, b * P - lo)
        nc.sync.dma_start(src_t[:], src)
        nc.sync.dma_start(dst_t[:], dst)

        x_bf = keep.tile([P, PACK * S], BF16, name="x_bf", align_bytes=64)
        x_slots = x_bf[:].rearrange("p (n j) -> p n j", j=PACK)
        x_codes = keep.tile([P, S], U32, name="x_codes", align_bytes=64)
        x_scales = keep.tile([P, S], U8, name="x_scales", align_bytes=64)
        early = keep.tile([P, 2, S], BF16, name="early")
        late = keep.tile([P, 2 * (S - DIRECT)], BF16, name="late")
        late_planes = late[:].rearrange("p (e n) -> p e n", e=2)

        res = {}
        res[E, 0] = keep.tile([P, S + COPY_SPARE], F32, name="e0")
        res[Y, 0] = reuse.tile([P, S + SPARE], F32, name="y0", offset=0, align_bytes=64)
        res[E, 1] = reuse.tile([P, S + SPARE], F32, name="e1", offset=8192, align_bytes=64)
        res[Y, 1] = keep.tile([P, S + SPARE], F32, name="y1")
        zeros = keep.tile([P, COPY_SPARE], F32, name="zeros")
        nc.gpsimd.memset(zeros[:], 0.0)
        for window in res.values():
            nc.scalar.activation(window[:, S:], zeros[:, : window.shape[1] - S], TANH)

        def pick_v(dest, j, lo, hi):
            nc.vector.tensor_copy(out=dest, in_=rows[j][:].indirect(entries(offs_t, lo, hi)))

        def pick_s(dest, j, lo, hi):
            nc.scalar.activation(dest, rows[j][:].indirect(entries(offs_t, lo, hi)), COPY)

        def insert(planes, first, lo, hi, copy=nc.vector.tensor_copy):
            copy(x_slots[:, lo:hi, first : first + 2], planes.rearrange("p e n -> p n e"))

        def insert_late(lo, hi, copy=nc.vector.tensor_copy):
            insert(late_planes[:, :, lo - DIRECT : hi - DIRECT], 2, lo, hi, copy)

        def quantise_x(lo, hi):
            nc.vector.quantize_mx(
                out=x_codes[:, lo:hi].bitcast(FP8X4), scales=x_scales[:, lo:hi], in_=x_bf[:, PACK * lo : PACK * hi]
            )

        w_codes = {}
        w_scales = {}

        def grouped_views(dest, i, b):
            grouped = dest.rearrange("p (c n j) -> p c j n", n=4, j=PACK)
            raw, first = w_raw[i, b]
            return grouped, raw[:, :, first : first + dest.shape[1] // PACK].rearrange("p j (c n) -> p c j n", n=4)

        def quantise_w(source, blocks, codes=None):
            width = P * len(blocks)
            if codes is None:
                codes = keep.tile([P, width], U32, name="w_codes%d_%d" % blocks[0], align_bytes=64)
            scales = keep.tile([P, width], U8, name="w_scales%d_%d" % blocks[0], align_bytes=64)
            nc.vector.quantize_mx(out=codes[:].bitcast(FP8X4), scales=scales[:], in_=source)
            for place, block in enumerate(blocks):
                w_codes[block] = codes[:, P * place : P * (place + 1)]
                w_scales[block] = scales[:, P * place : P * (place + 1)]

        def product(i, b, first, last, bank, width=512, copy=nc.scalar.copy):
            acc = psum.tile([P, last - first], F32, name="acc", tag="bank%d" % bank)
            for lo in range(first, last, width):
                hi = min(lo + width, last)
                nc.tensor.matmul_mx(
                    out=acc[:, lo - first : hi - first],
                    lhsT=w_codes[i, b].bitcast(FP8X4),
                    lhsT_scale=w_scales[i, b],
                    rhs=x_codes[:, lo:hi].bitcast(FP8X4),
                    rhs_scale=x_scales[:, lo:hi],
                    start=True,
                    stop=True,
                )
            copy(res[i, b][:, first:last], acc[:])

        def send(b, gate, lo, hi):
            message = keep.tile([P, hi - lo], F32, name="message%d_%d" % (b, lo))
            nc.vector.tensor_tensor(message[:], res[H, b][:].indirect(entries(src_t, lo, hi)), gate[:, lo:hi], MULT)
            nc.sync.dma_start(out=out[b * P : (b + 1) * P, lo:hi], in_=message[:])

        for j in range(2):
            pick_v(early[:, j, :512], j, 0, 512)
            pick_s(early[:, j, 512:], j, 512, S)
        insert(early[:], 0, 0, S)
        pick_v(x_slots[:, :DIRECT, 2], 2, 0, DIRECT)
        pick_s(late_planes[:, 0, :], 2, DIRECT, S)

        pick_v(x_slots[:, :DIRECT, 3], 3, 0, DIRECT)
        for lo, hi in LATE_PICKS:
            pick_s(late_planes[:, 1, lo - DIRECT : hi - DIRECT], 3, lo, hi)
        we_bf = [keep.tile([P, PACK * P], BF16, name="we_bf%d" % b, align_bytes=64) for b in range(2)]
        insert_late(*STEPS[2], nc.scalar.copy)
        nc.scalar.copy(*grouped_views(we_bf[1][:], E, 1))

        nc.vector.tensor_copy(*grouped_views(we_bf[0][:], E, 0))
        quantise_x(*STEPS[0])
        insert_late(*STEPS[1])
        quantise_w(we_bf[0][:], [(E, 0)])
        insert_late(*STEPS[3])
        quantise_x(*STEPS[1])
        quantise_x(*STEPS[3])
        quantise_x(*STEPS[2])
        quantise_w(we_bf[1][:], [(E, 1)])
        wy0_bf = keep.tile([P, PACK * P], BF16, name="wy0_bf", align_bytes=64)
        wh_bf = keep.tile([P, PACK * N], BF16, name="wh_bf", align_bytes=64)
        wy1_bf = wh_bf[:, PACK * P :]
        nc.vector.tensor_copy(*grouped_views(wy0_bf[:], Y, 0))
        nc.vector.tensor_copy(*grouped_views(wy1_bf, Y, 1))
        nc.vector.tensor_copy(*grouped_views(wh_bf[:, : PACK * VECTOR_COLUMNS], H, 0))
        quantise_w(wy0_bf[:], [(Y, 0)])
        quantise_w(wy1_bf, [(Y, 1)])

        for bank, step in enumerate((0, 1, 3, 2)):
            product(E, 0, *STEPS[step], bank)
        fetched = [keep.tile([P, U], F32, name="fetched%d" % b) for b in range(2)]
        nc.vector.tensor_copy(out=fetched[0][:], in_=res[E, 0][:].indirect(src_t[:]))

        nc.gpsimd.tensor_scalar(
            wh_bf[:, PACK * VECTOR_COLUMNS :].rearrange("p (n j) -> p n j", j=PACK),
            w_raw[H, 0][0][:, :, VECTOR_COLUMNS:].rearrange("p j n -> p n j"),
            1.0,
            0.0,
            MULT,
            ADD,
        )
        quantise_w(wh_bf[:], [(H, 0), (H, 1)])

        for step, (lo, hi) in enumerate(STEPS):
            product(E, 1, lo, hi, 4 + step)
        product(Y, 0, *STEPS[0], 0)
        product(Y, 0, *STEPS[1], 1)
        product(Y, 0, *HALVES[1], 2)
        product(Y, 1, *HALVES[0], 3)
        product(Y, 1, *STEPS[2], 4)
        product(Y, 1, *STEPS[3], 5, copy=nc.vector.tensor_copy)
        nc.scalar.activation(fetched[1][:], res[E, 1][:].indirect(src_t[:]), COPY)
        summed0 = reuse.tile([P, U], F32, name="summed0", offset=16384, align_bytes=64)
        summed1 = keep.tile([P, U], F32, name="summed1")
        nc.vector.tensor_tensor(summed0[:], res[Y, 0][:].indirect(dst_t[:]), fetched[0][:], ADD)
        nc.vector.tensor_tensor(summed1[:], res[Y, 1][:].indirect(dst_t[:]), fetched[1][:], ADD)

        res[H, 0] = keep.tile([P, S], F32, name="h0")
        product(H, 0, *HALVES[0], 4)
        product(H, 0, *HALVES[1], 3)
        gate0 = reuse.tile([P, U], F32, name="gate0", offset=8192, align_bytes=64)
        for lo, hi in HALVES:
            nc.scalar.activation(gate0[:, lo:hi], summed0[:, lo:hi], TANH)
            send(0, gate0, lo, hi)

        res[H, 1] = reuse.tile([P, S], F32, name="h1", offset=0, align_bytes=64)
        product(H, 1, *HALVES[0], 7)
        product(H, 1, *HALVES[1], 6)
        gate1 = keep.tile([P, U], F32, name="gate1")
        lo, hi = PLAIN
        nc.scalar.activation(gate1[:, :lo], summed1[:, :lo], TANH)
        nc.scalar.activation(gate1[:, lo:], summed1[:, lo:], TANH)
        send(1, gate1, 0, lo)
        at_src = keep.tile([P, hi - lo], F32, name="at_src")
        nc.scalar.activation(at_src[:], res[H, 1][:].indirect(entries(src_t, lo, hi)), COPY)
        message = keep.tile([P, hi - lo], F32, name="plain_message")
        nc.vector.tensor_tensor(message[:], at_src[:], gate1[:, lo:hi], MULT)
        nc.sync.dma_start(out=out[P:, lo:hi], in_=message[:])
        send(1, gate1, hi, U)
